import numpy as np
import ml_dtypes


def mxq(x, axis, fmt="e4m3"):
    dtype, down = {"e4m3": (ml_dtypes.float8_e4m3fn, 7), "e5m2": (ml_dtypes.float8_e5m2, 14)}[fmt]
    v = np.moveaxis(np.asarray(x, np.float32).astype(ml_dtypes.bfloat16).astype(np.float64), axis, -1)
    blocks = v.reshape(v.shape[:-1] + (-1, 32))
    amax = np.abs(blocks).max(-1, keepdims=True)
    byte = np.maximum(np.where(amax > 0, np.frexp(amax)[1] - 1 + 127, 0) - down, 1)
    scale = np.exp2(byte - 127.0)
    codes = (blocks / scale).astype(np.float32).astype(dtype).astype(np.float64)
    return np.moveaxis((codes * scale).reshape(v.shape), -1, axis)


WIDE = False


def mx_kscale(k):
    if not WIDE:
        return np.ones(k)
    levels = np.array([10, -10, 5, -5, 0])
    if k % 512:
        return np.exp2(np.random.permutation(np.resize(levels, k // 32))).repeat(32)
    a = np.empty((k // 512, 16))
    for p in range(k // 512):
        a[p, :8] = np.random.permutation(np.resize(levels, 8))
        for g in range(8):
            far = levels[np.abs(levels - a[p, g]) >= 10]
            a[p, g + 8] = far[np.random.randint(len(far))]
    return np.exp2(a.ravel()).repeat(32)


BF16 = ml_dtypes.bfloat16


def bf(x):
    return np.asarray(x, np.float32).astype(BF16)


def f64(x):
    return np.asarray(x).astype(np.float64)


E2M1 = np.array([0.0, 0.5, 1.0, 1.5, 2.0, 3.0, 4.0, 6.0, -0.0, -0.5, -1.0, -1.5, -2.0, -3.0, -4.0, -6.0])


def pack_weight(w, fmt):
    k, n = w.shape
    w = f64(bf(w)).reshape(k // 32, 32, n)
    amax = np.abs(w).max(1)
    if fmt == "e4m3":
        byte = np.frexp(amax)[1] - 1 + 127 - 7
    else:
        mant, ex = np.frexp(amax / 6.0)
        byte = np.where(mant > 0.5, ex, ex - 1) + 127
    byte = np.clip(np.where(amax > 0, byte, 1), 1, 254)
    scaled = (w * np.exp2(127.0 - byte)[:, None, :]).reshape(k, n).astype(np.float32)
    by_word = np.ascontiguousarray(scaled.reshape(k // 512, 128, 4, n).transpose(0, 1, 3, 2))
    if fmt == "e4m3":
        words = by_word.astype(ml_dtypes.float8_e4m3fn).view(np.uint8)
    else:
        c = by_word.astype(ml_dtypes.float4_e2m1fn).view(np.uint8) & 0xF
        words = c[..., 0::2] | (c[..., 1::2] << 4)
    return np.ascontiguousarray(words), np.ascontiguousarray(byte.astype(np.uint8).reshape(k // 512, 16, n))


def unpack_weight(words, scales, fmt):
    g, p, n, _ = words.shape
    if fmt == "e4m3":
        vals = np.ascontiguousarray(words).view(ml_dtypes.float8_e4m3fn).astype(np.float64)
    else:
        nib = np.empty((g, p, n, 4), np.uint8)
        nib[..., 0::2] = words & 0xF
        nib[..., 1::2] = words >> 4
        vals = E2M1[nib]
    vals = vals * np.repeat(np.exp2(scales.astype(np.float64) - 127.0), 8, axis=1)[..., None]
    return vals.transpose(0, 1, 3, 2).reshape(g * 512, n)
def pack4(w):
    words, scales = pack_weight(w, "e2m1")
    return words.reshape(words.shape[0], 128, -1), scales


def unpack4(words, scales):
    return unpack_weight(words.reshape(words.shape[0], 128, -1, 2), scales, "e2m1")


def planes(Y):
    n, m = Y.shape
    b = f64(bf(Y)).reshape(n // 32, 32, m)
    amax = np.abs(b).max(1)
    byte = np.clip(np.where(amax > 0, np.frexp(amax)[1] - 1 + 127 - 7, 1), 1, 254)
    codes = (b * np.exp2(127.0 - byte)[:, None, :]).reshape(n, m).astype(np.float32).astype(ml_dtypes.float8_e4m3fn).view(np.uint8)
    words = codes.reshape(n // 512, 128, 4, m).transpose(0, 1, 3, 2)
    return np.ascontiguousarray(words), np.ascontiguousarray(byte.astype(np.uint8).reshape(n // 512, 16, m))


B, NO, NV, NF, G = 512, 512, 512, 1024, 2048
AMP = 1.5

def setup_inputs():
    rn, un = np.random.randn, np.random.uniform
    so, sv, sf, t = mx_kscale(NO), mx_kscale(NV), mx_kscale(NF), mx_kscale(G)
    xo_b = bf(AMP * rn(NO, B) * so[:, None])
    xo_g = bf(rn(NO, G) / np.sqrt(NO) / so[:, None] * t[None, :])
    xv_b = bf(AMP * rn(NV, B) * sv[:, None])
    xv_g = bf(rn(NV, G) / np.sqrt(NV) / sv[:, None])
    xf_b = bf(AMP * rn(NF, B) * sf[:, None])
    xf_words, xf_scales = pack4(rn(NF, G) / np.sqrt(NV) / sf[:, None])
    eo, ev, ef = bf(un(0.1, 1.0, NO)), bf(un(0.1, 1.0, NV)), bf(un(0.8, 1.6, NF))
    c_words, c_scales = pack_weight(rn(G, G) / np.sqrt(G) / t[:, None], "e4m3")
    w = bf(np.exp(0.8 * rn(G)))
    return {"xo_b": xo_b, "xo_g": xo_g, "eo": eo, "xv_b": xv_b, "xv_g": xv_g, "ev": ev,
            "xf_b": xf_b, "xf_words": xf_words, "xf_scales": xf_scales, "ef": ef,
            "c_words": c_words, "c_scales": c_scales, "w": w}

def reference(xo_b, xo_g, eo, xv_b, xv_g, ev, xf_b, xf_words, xf_scales, ef, c_words, c_scales, w):
    lo = mxq(f64(xo_b) * np.exp(-f64(eo))[:, None], 0, "e4m3")
    lv = mxq(f64(xv_b) * np.exp(-f64(ev))[:, None], 0, "e4m3")
    lf = mxq(f64(xf_b) * np.exp(-f64(ef))[:, None], 0, "e4m3")
    occ = lo.T @ mxq(f64(xo_g), 0, "e4m3")
    vir = (lv.T @ mxq(f64(xv_g), 0, "e4m3")) + (lf.T @ unpack4(xf_words, xf_scales))
    h = occ * vir
    y = (mxq(h, 1, "e4m3") @ unpack_weight(c_words, c_scales, "e4m3")) * f64(w)[None, :]
    Y = y.T
    words, scales = planes(Y)
    return y, words, scales

@@ -1,0 +1,546 @@
+from contextlib import ExitStack
+
+import concourse.mybir as mybir
+from concourse.masks import make_identity
+
+F32 = mybir.dt.float32
+BF16 = mybir.dt.bfloat16
+I32 = mybir.dt.int32
+U32 = mybir.dt.uint32
+U8 = mybir.dt.uint8
+FP8X4 = mybir.dt.float8_e4m3fn_x4
+FP4X4 = mybir.dt.float4_e2m1fn_x4
+MULT = mybir.AluOpType.mult
+EXP = mybir.ActivationFunctionType.Exp
+
+P = 128
+PACK = 4
+W = 512
+NCH = 4
+NB = 4
+QUADS = 4
+ACC_BANKS = 6
+TP_BANKS = 2
+ORDER = [
+    ('lx', 0, 0),
+    ('ll', 0),
+    ('lx', 0, 1),
+    ('ll', 1),
+    ('ll', 2),
+    ('ls', 0),
+    ('lf', 0),
+    ('ll', 3),
+    ('lx', 1, 0),
+    ('lx', 1, 1),
+    ('ls', 1),
+    ('lf', 1),
+    ('lx', 2, 0),
+    ('lx', 2, 1),
+    ('lf', 2),
+    ('lx', 3, 0),
+    ('lx', 3, 1),
+    ('lf', 3),
+    ('lcs',),
+    ('lc', 0),
+    ('lw',),
+    ('lc', 1),
+    ('lc', 2),
+    ('lc', 3),
+    ('il', ('x', 0, 0), True, 0, 256),
+    ('il', ('x', 0, 0), False, 256, 512),
+    ('sl', 0, 0, 512),
+    ('il', ('l', 0), True, 0, 256),
+    ('qx', 0, 0),
+    ('il', ('l', 0), False, 256, 512),
+    ('il', ('x', 0, 1), True, 0, 256),
+    ('il', ('x', 0, 1), False, 256, 512),
+    ('sl', 1, 0, 512),
+    ('il', ('l', 1), True, 0, 512),
+    ('ql', 0, 0, 512),
+    ('m1', 0, 0, 0),
+    ('m1', 0, 1, 0),
+    ('m1', 0, 2, 0),
+    ('m1', 0, 3, 0),
+    ('sl', 2, 0, 512),
+    ('qx', 0, 1),
+    ('il', ('l', 2), False, 128, 512),
+    ('co', 0, 0),
+    ('co', 0, 1),
+    ('il', ('l', 2), True, 0, 128),
+    ('ql', 1, 0, 512),
+    ('m1', 0, 0, 1),
+    ('m1', 0, 1, 1),
+    ('m1', 0, 2, 1),
+    ('m1', 0, 3, 1),
+    ('sl', 3, 0, 512),
+    ('ql', 2, 0, 512),
+    ('il', ('x', 1, 0), True, 0, 384),
+    ('co', 0, 2),
+    ('co', 0, 3),
+    ('m1', 0, 0, 2),
+    ('m1', 0, 1, 2),
+    ('m1', 0, 2, 2),
+    ('m1', 0, 3, 2),
+    ('il', ('l', 3), False, 0, 256),
+    ('il', ('l', 3), False, 256, 512),
+    ('ql', 3, 0, 256),
+    ('il', ('x', 1, 0), False, 384, 512),
+    ('ql', 3, 256, 512),
+    ('il', ('x', 1, 1), True, 0, 384),
+    ('m1', 0, 0, 3),
+    ('m1', 0, 1, 3),
+    ('m1', 0, 2, 3),
+    ('m1', 0, 3, 3),
+    ('il', ('x', 1, 1), False, 384, 512),
+    ('qx', 1, 0),
+    ('mh', 0, 0),
+    ('qx', 1, 1),
+    ('mh', 0, 1),
+    ('m1', 1, 0, 0),
+    ('m1', 1, 0, 2),
+    ('m1', 1, 0, 3),
+    ('m1', 1, 0, 1),
+    ('co', 1, 0),
+    ('mh', 0, 2),
+    ('mh', 0, 3),
+    ('il', ('x', 2, 0), True, 0, 320),
+    ('il', ('x', 2, 0), False, 320, 512),
+    ('mh', 1, 0),
+    ('m1', 1, 1, 0),
+    ('m1', 1, 1, 2),
+    ('m1', 1, 1, 3),
+    ('m1', 1, 1, 1),
+    ('co', 1, 1),
+    ('tp', 'h', 0, (0, 1)),
+    ('tp', 'h', 0, (2, 3)),
+    ('qx', 2, 0),
+    ('mh', 1, 1),
+    ('il', ('x', 2, 1), True, 0, 320),
+    ('il', ('x', 2, 1), False, 320, 512),
+    ('m1', 1, 2, 0),
+    ('m1', 1, 2, 2),
+    ('m1', 1, 2, 3),
+    ('m1', 1, 2, 1),
+    ('co', 1, 2),
+    ('ct', 'h', 0, (0, 1)),
+    ('mh', 1, 2),
+    ('qx', 2, 1),
+    ('m1', 1, 3, 0),
+    ('m1', 1, 3, 2),
+    ('m1', 1, 3, 3),
+    ('m1', 1, 3, 1),
+    ('co', 1, 3),
+    ('ct', 'h', 0, (2, 3)),
+    ('qh', 0, (0, 1)),
+    ('m1', 2, 0, 0),
+    ('m1', 2, 0, 2),
+    ('m1', 2, 0, 3),
+    ('m1', 2, 0, 1),
+    ('co', 2, 0),
+    ('mh', 1, 3),
+    ('qh', 0, (2, 3)),
+    ('il', ('x', 3, 0), True, 0, 256),
+    ('il', ('x', 3, 0), False, 256, 512),
+    ('mh', 2, 0),
+    ('m1', 2, 1, 0),
+    ('m1', 2, 1, 2),
+    ('m1', 2, 1, 3),
+    ('m1', 2, 1, 1),
+    ('co', 2, 1),
+    ('tp', 'h', 1, (0, 1)),
+    ('tp', 'h', 1, (2, 3)),
+    ('qx', 3, 0),
+    ('mh', 2, 1),
+    ('il', ('x', 3, 1), True, 0, 256),
+    ('il', ('x', 3, 1), False, 256, 512),
+    ('m1', 2, 2, 0),
+    ('m1', 2, 2, 2),
+    ('m1', 2, 2, 3),
+    ('m1', 2, 2, 1),
+    ('co', 2, 2),
+    ('ct', 'h', 1, (0, 1)),
+    ('mh', 2, 2),
+    ('qx', 3, 1),
+    ('m1', 2, 3, 0),
+    ('m1', 2, 3, 2),
+    ('m1', 2, 3, 3),
+    ('m1', 2, 3, 1),
+    ('co', 2, 3),
+    ('ct', 'h', 1, (2, 3)),
+    ('qh', 1, (0, 1)),
+    ('m1', 3, 0, 0),
+    ('m1', 3, 0, 2),
+    ('m1', 3, 0, 3),
+    ('m1', 3, 0, 1),
+    ('co', 3, 0),
+    ('mh', 2, 3),
+    ('qh', 1, (2, 3)),
+    ('mh', 3, 0),
+    ('m1', 3, 1, 0),
+    ('m1', 3, 1, 2),
+    ('m1', 3, 1, 3),
+    ('m1', 3, 1, 1),
+    ('co', 3, 1),
+    ('tp', 'h', 2, (0, 1)),
+    ('tp', 'h', 2, (2, 3)),
+    ('mh', 3, 1),
+    ('m1', 3, 2, 0),
+    ('m1', 3, 2, 2),
+    ('m1', 3, 2, 3),
+    ('m1', 3, 2, 1),
+    ('co', 3, 2),
+    ('ct', 'h', 2, (0, 1)),
+    ('mh', 3, 2),
+    ('m1', 3, 3, 0),
+    ('m1', 3, 3, 2),
+    ('m1', 3, 3, 3),
+    ('m1', 3, 3, 1),
+    ('co', 3, 3),
+    ('ct', 'h', 2, (2, 3)),
+    ('qh', 2, (0, 1)),
+    ('mh', 3, 3),
+    ('qh', 2, (2, 3)),
+    ('m2', 0, 0, (0, 1, 2)),
+    ('m2', 0, 1, (0, 1, 2)),
+    ('tp', 'h', 3, (0, 1)),
+    ('tp', 'h', 3, (2, 3)),
+    ('ct', 'h', 3, (0, 1)),
+    ('ct', 'h', 3, (2, 3)),
+    ('qh', 3, (0, 1)),
+    ('qh', 3, (2, 3)),
+    ('m2', 0, 2, (0, 1, 2)),
+    ('m2', 0, 3, (0, 1, 2)),
+    ('m2', 0, 0, (3,)),
+    ('my', 0, 0),
+    ('cy', 0, 0),
+    ('m2', 0, 1, (3,)),
+    ('my', 0, 1),
+    ('cy', 0, 1),
+    ('m2', 0, 2, (3,)),
+    ('my', 0, 2),
+    ('cy', 0, 2),
+    ('m2', 0, 3, (3,)),
+    ('my', 0, 3),
+    ('cy', 0, 3),
+    ('m2', 1, 0, (0, 1, 2, 3)),
+    ('m2', 1, 1, (0, 1, 2, 3)),
+    ('tp', 'y', 0, (0, 1)),
+    ('tp', 'y', 0, (2, 3)),
+    ('my', 1, 0),
+    ('ct', 'y', 0, (0, 1)),
+    ('ct', 'y', 0, (2, 3)),
+    ('cy', 1, 0),
+    ('my', 1, 1),
+    ('cy', 1, 1),
+    ('qy', 0, (0, 1)),
+    ('m2', 1, 2, (0, 1, 2, 3)),
+    ('my', 1, 2),
+    ('qy', 0, (2, 3)),
+    ('sw', 0, 0, 512),
+    ('cy', 1, 2),
+    ('m2', 1, 3, (0, 1, 2, 3)),
+    ('my', 1, 3),
+    ('cy', 1, 3),
+    ('m2', 2, 0, (0, 1, 2, 3)),
+    ('m2', 2, 1, (0, 1, 2, 3)),
+    ('tp', 'y', 1, (0, 1)),
+    ('tp', 'y', 1, (2, 3)),
+    ('my', 2, 0),
+    ('ct', 'y', 1, (0, 1)),
+    ('ct', 'y', 1, (2, 3)),
+    ('cy', 2, 0),
+    ('my', 2, 1),
+    ('cy', 2, 1),
+    ('qy', 1, (0, 1)),
+    ('m2', 2, 2, (0, 1, 2, 3)),
+    ('my', 2, 2),
+    ('qy', 1, (2, 3)),
+    ('sw', 1, 0, 512),
+    ('cy', 2, 2),
+    ('m2', 2, 3, (0, 1, 2, 3)),
+    ('my', 2, 3),
+    ('cy', 2, 3),
+    ('m2', 3, 0, (0, 1, 2, 3)),
+    ('m2', 3, 1, (0, 1, 2, 3)),
+    ('tp', 'y', 2, (0, 1)),
+    ('tp', 'y', 2, (2, 3)),
+    ('my', 3, 0),
+    ('ct', 'y', 2, (0, 1)),
+    ('ct', 'y', 2, (2, 3)),
+    ('cy', 3, 0),
+    ('my', 3, 1),
+    ('cy', 3, 1),
+    ('qy', 2, (0, 1)),
+    ('m2', 3, 2, (0, 1, 2, 3)),
+    ('my', 3, 2),
+    ('qy', 2, (2, 3)),
+    ('sw', 2, 0, 512),
+    ('cy', 3, 2),
+    ('m2', 3, 3, (0, 1, 2, 3)),
+    ('tp', 'y', 3, (0, 1)),
+    ('tp', 'y', 3, (2,)),
+    ('ct', 'y', 3, (0, 1)),
+    ('mb', 3, 3),
+    ('my', 3, 3),
+    ('ct', 'y', 3, (2,)),
+    ('tp', 'y', 3, (3,)),
+    ('qy', 3, (0, 1)),
+    ('ct', 'y', 3, (3,)),
+    ('qy', 3, (2,)),
+    ('sw', 3, 0, 384),
+    ('qy', 3, (3,)),
+    ('sw', 3, 384, 512),
+    ('ss',),
+]
+
+FLOPS = 2 * 512 * 2048 * (512 + 512 + 1024 + 2048)
+
+
+def tile_thc_laplace_mp2_core_product_k6_kernel(
+    tc, xo_b, xo_g, eo, xv_b, xv_g, ev, xf_b, xf_words, xf_scales, ef, c_words, c_scales, w,
+    out_0, out_1, out_2,
+):
+    nc = tc.nc
+    with ExitStack() as ctx:
+        sb = ctx.enter_context(tc.tile_pool(name="sb", bufs=1))
+        ps = ctx.enter_context(tc.psum_pool(name="ps", bufs=1))
+        ctx.enter_context(tc.manual_schedule())
+
+        turns = {}
+
+        def ring(pool, tag, depth, shape, dtype):
+            turn = turns.get(tag, 0)
+            turns[tag] = turn + 1
+            if pool is ps:
+                return pool.tile(shape, dtype, name="%s_%d" % (tag, turn), tag="%s%d" % (tag, turn % depth))
+            return pool.tile(shape, dtype, name="%s_%d" % (tag, turn), tag="%s%d" % (tag, turn % depth), align_bytes=64)
+
+        def keep(name, shape, dtype):
+            return sb.tile(shape, dtype, name=name, align_bytes=64)
+
+        def chunk(c):
+            return slice(c * W, (c + 1) * W)
+
+        ident = keep("ident", [P, P], F32)
+        make_identity(nc, ident[:])
+
+        xf_sc0 = keep("xf_sc0", [P, 2, W], U8)
+        xf_sc1 = keep("xf_sc1", [P, 2, (NCH - 1) * W], U8)
+        c_sc = keep("c_sc", [P, NCH * W], U8)
+        nc.vector.memset(xf_sc0[:].rearrange("p g n -> p (g n)").bitcast(U32), 0)
+        nc.vector.memset(xf_sc1[:].rearrange("p g n -> p (g n)").bitcast(U32), 0)
+        nc.vector.memset(c_sc[:].bitcast(U32), 0)
+
+        eo_sb = keep("eo_sb", [P, PACK], BF16)
+        ev_sb = keep("ev_sb", [P, PACK], BF16)
+        ef_sb = keep("ef_sb", [P, 2, PACK], BF16)
+        nc.scalar.dma_start(out=eo_sb[:], in_=eo.rearrange("(p j) -> p j", j=PACK))
+        nc.scalar.dma_start(out=ev_sb[:], in_=ev.rearrange("(p j) -> p j", j=PACK))
+        nc.scalar.dma_start(out=ef_sb[:], in_=ef.rearrange("(g p j) -> p g j", g=2, j=PACK))
+        damp = keep("damp", [P, 4 * PACK], F32)
+        nc.scalar.activation(out=damp[:, 0:4], in_=eo_sb[:], func=EXP, scale=-1.0)
+        nc.scalar.activation(out=damp[:, 4:8], in_=ev_sb[:], func=EXP, scale=-1.0)
+        nc.scalar.activation(out=damp[:, 8:16], in_=ef_sb[:].rearrange("p g j -> p (g j)"), func=EXP, scale=-1.0)
+
+        l_src = [xo_b, xv_b, xf_b[0:W, :], xf_b[W : 2 * W, :]]
+        x_src = [xo_g, xv_g]
+        l_raw, x_raw, xf_w, c_w, src_of, grouped = {}, {}, {}, {}, {}, {}
+
+        def load_l(k):
+            l_raw[k] = keep("l_raw%d" % k, [P, PACK, W], BF16)
+            nc.sync.dma_start(out=l_raw[k][:], in_=l_src[k].rearrange("(p j) b -> p j b", j=PACK))
+
+        def load_x(g, s):
+            x_raw[g, s] = keep("x_raw%d_%d" % (g, s), [P, PACK, W], BF16)
+            src_of["x", g, s] = x_raw[g, s]
+            nc.sync.dma_start(out=x_raw[g, s][:], in_=x_src[s][:, chunk(g)].rearrange("(p j) n -> p j n", j=PACK))
+
+        def load_xf(g):
+            xf_w[g] = keep("xf_w%d" % g, [P, 2, 2 * W], U8)
+            src = xf_words.rearrange("k p n -> p k n")[:, :, 2 * W * g : 2 * W * (g + 1)]
+            nc.sync.dma_start(out=xf_w[g][:].bitcast(I32), in_=src.bitcast(I32))
+
+        def load_c(n):
+            c_w[n] = keep("c_w%d" % n, [P, NCH, W], U32)
+            src = c_words.rearrange("g p n t -> p g (n t)")[:, :, PACK * W * n : PACK * W * (n + 1)]
+            nc.sync.dma_start(out=c_w[n][:].bitcast(I32), in_=src.bitcast(I32))
+
+        def load_xf_scales(plane, cols):
+            for q in range(QUADS):
+                nc.sync.dma_start(
+                    out=plane[32 * q : 32 * q + 4, :, :].bitcast(I32),
+                    in_=xf_scales[:, 4 * q : 4 * q + 4, cols].rearrange("k r n -> r k n").bitcast(I32),
+                )
+
+        def load_xs(i):
+            load_xf_scales(*[(xf_sc0, slice(0, W)), (xf_sc1, slice(W, NCH * W))][i])
+
+        def load_cs():
+            for q in range(QUADS):
+                nc.sync.dma_start(
+                    out=c_sc[32 * q : 32 * q + 16, :].bitcast(I32),
+                    in_=c_scales[:, 4 * q : 4 * q + 4, :].bitcast(I32),
+                )
+
+        w_sb = keep("w_sb", [P, NCH * W], BF16)
+
+        def load_w():
+            nc.sync.dma_start(out=w_sb[:], in_=w.partition_broadcast(P))
+
+        l_codes = keep("l_codes", [P, 4, W], U32)
+        l_sc = keep("l_sc", [P, 4, W], U8)
+        x_codes = keep("x_codes", [P, NCH, 2, W], U32)
+        x_sc = keep("x_sc", [P, NCH, 2, W], U8)
+        h_codes = keep("h_codes", [P, NCH, W], U32)
+        h_sc = keep("h_sc", [P, NCH, W], U8)
+        y_sc = keep("y_sc", [P, W], U8)
+
+        def scale_l(k, c0, c1):
+            if ("l", k) not in src_of:
+                src_of["l", k] = ring(sb, "damped", 3, [P, PACK, W], BF16)
+            for j in range(PACK):
+                nc.vector.tensor_scalar(
+                    out=src_of["l", k][:, j, c0:c1], in0=l_raw[k][:, j, c0:c1],
+                    scalar1=damp[:, PACK * k + j : PACK * k + j + 1], scalar2=None, op0=MULT,
+                )
+
+        def interleave(key, on_scalar, c0, c1):
+            if key not in grouped:
+                grouped[key] = ring(sb, "grouped", 5, [P, W, PACK], BF16)
+            dst = grouped[key][:, c0:c1, :].rearrange("p (c i) t -> p c t i", i=4)
+            src = src_of[key][:, :, c0:c1].rearrange("p t (c i) -> p c t i", i=4)
+            if on_scalar:
+                nc.scalar.copy(out=dst, in_=src)
+            else:
+                nc.vector.tensor_copy(out=dst, in_=src)
+
+        def quantize(codes, scales, values):
+            nc.vector.quantize_mx(out=codes.bitcast(FP8X4), scales=scales, in_=values)
+
+        def quant_l(k, c0, c1):
+            quantize(l_codes[:, k, c0:c1], l_sc[:, k, c0:c1], grouped["l", k][:, c0:c1, :].rearrange("p n t -> p (n t)"))
+
+        def quant_x(g, s):
+            quantize(x_codes[:, g, s, :], x_sc[:, g, s, :], grouped["x", g, s][:].rearrange("p n t -> p (n t)"))
+
+        o_ps, v_ps, o_sb, y_ps, y_sb, paired, turned = {}, {}, {}, {}, {}, {}, {}
+
+        v_done = {}
+
+        def rows(b):
+            return slice(b * P, (b + 1) * P)
+
+        def mm1(g, b, k):
+            if k == 0:
+                o_ps[g, b] = ring(ps, "acc", ACC_BANKS, [P, W], F32)
+            if k > 0:
+                v_done[g, b] = v_done.get((g, b), 0) + 1
+            if k > 0 and v_done[g, b] == 1:
+                v_ps[g, b] = ring(ps, "acc", ACC_BANKS, [P, W], F32)
+            if k < 2:
+                rhs, rhs_scale = x_codes[:, g, k, :].bitcast(FP8X4), x_sc[:, g, k, :]
+            else:
+                rhs, rhs_scale = xf_w[g][:, k - 2, :].bitcast(FP4X4), (xf_sc1[:, k - 2, chunk(g - 1)] if g else xf_sc0[:, k - 2, :])
+            nc.tensor.matmul_mx(
+                out=(o_ps if k == 0 else v_ps)[g, b][:],
+                lhsT=l_codes[:, k, rows(b)].bitcast(FP8X4), lhsT_scale=l_sc[:, k, rows(b)],
+                rhs=rhs, rhs_scale=rhs_scale, start=(k == 0 or v_done[g, b] == 1), stop=(k == 0 or v_done[g, b] == 3),
+            )
+
+        def mm1_tile(g, b):
+            for k in range(4):
+                mm1(g, b, k)
+
+        def by_pairs(ap):
+            return ap.rearrange("p (m u e) -> p u m e", u=2, e=2)
+
+        def as_pairs(ap):
+            return ap.rearrange("p (u m e) -> p u m e", u=2, e=2)
+
+        def copy_o(g, b):
+            o_sb[g, b] = ring(sb, "o_sb", 6, [P, W], F32)
+            nc.scalar.copy(out=as_pairs(o_sb[g, b][:]), in_=by_pairs(o_ps[g, b][:]))
+
+        def mul_h(g, b):
+            paired["h", g, b] = ring(sb, "paired", 8, [P, W], BF16)
+            nc.vector.tensor_tensor(
+                out=as_pairs(paired["h", g, b][:]), in0=by_pairs(v_ps[g, b][:]), in1=as_pairs(o_sb[g, b][:]), op=MULT,
+            )
+
+        def turn(kind, c, bs):
+            bank = ring(ps, "tp", TP_BANKS, [P, 4, P], F32)
+            for i, b in enumerate(bs):
+                words = paired[kind, c, b][:].bitcast(F32)
+                for u in range(2):
+                    nc.tensor.transpose(bank[:, 2 * i + u, :], words[:, u * P : (u + 1) * P], ident[:])
+            turned[kind, c, bs] = bank
+
+        def copy_turned(kind, c, bs):
+            bank = turned[kind, c, bs]
+            dst = ring(sb, "kfirst", 4, [P, 2 * W], BF16)
+            nb = len(bs)
+            nc.scalar.copy(
+                out=dst[:, 0 : nb * W].bitcast(F32).rearrange("p (i r u) -> p i r u", i=nb, u=2),
+                in_=bank[:, 0 : 2 * nb, :].rearrange("p (i u) r -> p i r u", u=2),
+            )
+            turned[kind, c, bs] = dst
+
+        def quant_h(g, bs):
+            cols = slice(bs[0] * P, (bs[-1] + 1) * P)
+            quantize(h_codes[:, g, cols], h_sc[:, g, cols], turned["h", g, bs][:, 0 : len(bs) * W])
+
+        y_codes = {}
+
+        def mm2(n, b, gs):
+            for g in gs:
+                if g == 0:
+                    y_ps[n, b] = ring(ps, "acc", ACC_BANKS, [P, W], F32)
+                nc.tensor.matmul_mx(
+                    out=y_ps[n, b][:],
+                    lhsT=h_codes[:, g, rows(b)].bitcast(FP8X4), lhsT_scale=h_sc[:, g, rows(b)],
+                    rhs=c_w[n][:, g, :].bitcast(FP8X4), rhs_scale=c_sc[4 * g :, chunk(n)],
+                    start=(g == 0), stop=(g == NCH - 1),
+                )
+
+        def mul_y(n, b):
+            y_sb[n, b] = ring(sb, "y_sb", 8, [P, W], F32)
+            nc.vector.tensor_tensor(out=y_sb[n, b][:], in0=y_ps[n, b][:], in1=w_sb[:, chunk(n)], op=MULT)
+            nc.sync.dma_start(out=out_0[rows(b), chunk(n)], in_=y_sb[n, b][:])
+
+        def cast_y(n, b):
+            paired["y", n, b] = ring(sb, "paired", 8, [P, W], BF16)
+            nc.scalar.copy(out=as_pairs(paired["y", n, b][:]), in_=by_pairs(y_sb[n, b][:]))
+
+        def quant_y(n, bs):
+            if n not in y_codes:
+                y_codes[n] = keep("y_codes%d" % n, [P, W], U32)
+            cols = slice(bs[0] * P, (bs[-1] + 1) * P)
+            quantize(y_codes[n][:, cols], y_sc[4 * n :, cols], turned["y", n, bs][:, 0 : len(bs) * W])
+
+        def store_words(n, c0, c1):
+            cols = slice(c0, c1)
+            dst = out_1[n].rearrange("p m t -> p (m t)").bitcast(I32)
+            nc.sync.dma_start(out=dst[:, cols], in_=y_codes[n][:, cols].bitcast(I32))
+
+        def mul_y_bf16(n, b):
+            paired["y", n, b] = ring(sb, "paired", 8, [P, W], BF16)
+            nc.vector.tensor_tensor(
+                out=as_pairs(paired["y", n, b][:]), in0=by_pairs(y_ps[n, b][:]), in1=by_pairs(w_sb[:, chunk(n)]), op=MULT,
+            )
+
+        def store_scales():
+            for q in range(QUADS):
+                eng = nc.sync if q % 2 else nc.scalar
+                eng.dma_start(
+                    out=out_2[:, 4 * q : 4 * q + 4, :].bitcast(I32),
+                    in_=y_sc[32 * q : 32 * q + 16, :].bitcast(I32),
+                )
+
+        steps = {
+            "sl": scale_l, "il": interleave, "ql": quant_l, "qx": quant_x, "m1": mm1, "co": copy_o, "mh": mul_h,
+            "tp": turn, "ct": copy_turned, "qh": quant_h, "m2": mm2, "my": mul_y, "cy": cast_y, "qy": quant_y,
+            "lx": load_x, "ll": load_l, "lf": load_xf, "lc": load_c, "ls": load_xs, "lcs": load_cs, "lw": load_w,
+            "sw": store_words, "mb": mul_y_bf16, "ss": store_scales,
+        }
+        for step in ORDER:
+            steps[step[0]](*step[1:])

@@ -19,189 +19,191 @@ W = 512
 NCH = 4
 NB = 4
 QUADS = 4
-ACC_BANKS = 6
-TP_BANKS = 2
+BANKS = 8
+COPY_V = True
 ORDER = [
-    ('lx', 0, 0),
-    ('ll', 0),
-    ('lx', 0, 1),
-    ('ll', 1),
     ('ll', 2),
+    ('ll', 3),
+    ('ll', 1),
     ('ls', 0),
     ('lf', 0),
-    ('ll', 3),
-    ('lx', 1, 0),
-    ('lx', 1, 1),
+    ('lx', 0, 1),
+    ('lx', 0, 0),
+    ('ll', 0),
     ('ls', 1),
     ('lf', 1),
-    ('lx', 2, 0),
-    ('lx', 2, 1),
+    ('lx', 1, 1),
+    ('lx', 1, 0),
+    ('ls', 2),
     ('lf', 2),
-    ('lx', 3, 0),
-    ('lx', 3, 1),
+    ('lx', 2, 1),
+    ('lx', 2, 0),
+    ('ls', 3),
     ('lf', 3),
+    ('lx', 3, 1),
+    ('lx', 3, 0),
     ('lcs',),
     ('lc', 0),
     ('lw',),
     ('lc', 1),
     ('lc', 2),
     ('lc', 3),
-    ('il', ('x', 0, 0), True, 0, 256),
-    ('il', ('x', 0, 0), False, 256, 512),
-    ('sl', 0, 0, 512),
-    ('il', ('l', 0), True, 0, 256),
-    ('qx', 0, 0),
-    ('il', ('l', 0), False, 256, 512),
-    ('il', ('x', 0, 1), True, 0, 256),
-    ('il', ('x', 0, 1), False, 256, 512),
-    ('sl', 1, 0, 512),
-    ('il', ('l', 1), True, 0, 512),
-    ('ql', 0, 0, 512),
-    ('m1', 0, 0, 0),
-    ('m1', 0, 1, 0),
-    ('m1', 0, 2, 0),
-    ('m1', 0, 3, 0),
     ('sl', 2, 0, 512),
-    ('qx', 0, 1),
-    ('il', ('l', 2), False, 128, 512),
-    ('co', 0, 0),
-    ('co', 0, 1),
-    ('il', ('l', 2), True, 0, 128),
-    ('ql', 1, 0, 512),
-    ('m1', 0, 0, 1),
-    ('m1', 0, 1, 1),
-    ('m1', 0, 2, 1),
-    ('m1', 0, 3, 1),
+    ('il', ('l', 2), True, 0, 256),
+    ('il', ('l', 2), False, 256, 512),
     ('sl', 3, 0, 512),
+    ('il', ('l', 3), True, 0, 256),
     ('ql', 2, 0, 512),
-    ('il', ('x', 1, 0), True, 0, 384),
-    ('co', 0, 2),
-    ('co', 0, 3),
     ('m1', 0, 0, 2),
     ('m1', 0, 1, 2),
     ('m1', 0, 2, 2),
     ('m1', 0, 3, 2),
-    ('il', ('l', 3), False, 0, 256),
+    ('sl', 1, 0, 512),
+    ('il', ('l', 1), True, 0, 256),
     ('il', ('l', 3), False, 256, 512),
-    ('ql', 3, 0, 256),
-    ('il', ('x', 1, 0), False, 384, 512),
-    ('ql', 3, 256, 512),
-    ('il', ('x', 1, 1), True, 0, 384),
+    ('il', ('l', 1), False, 256, 512),
+    ('ql', 3, 0, 512),
     ('m1', 0, 0, 3),
     ('m1', 0, 1, 3),
     ('m1', 0, 2, 3),
     ('m1', 0, 3, 3),
-    ('il', ('x', 1, 1), False, 384, 512),
-    ('qx', 1, 0),
-    ('mh', 0, 0),
-    ('qx', 1, 1),
-    ('mh', 0, 1),
-    ('m1', 1, 0, 0),
+    ('il', ('x', 0, 1), True, 0, 256),
+    ('il', ('x', 0, 1), False, 256, 512),
+    ('ql', 1, 0, 512),
+    ('qx', 0, 1),
+    ('m1', 0, 0, 1),
+    ('m1', 0, 1, 1),
+    ('m1', 0, 2, 1),
+    ('m1', 0, 3, 1),
     ('m1', 1, 0, 2),
     ('m1', 1, 0, 3),
-    ('m1', 1, 0, 1),
-    ('co', 1, 0),
-    ('mh', 0, 2),
-    ('mh', 0, 3),
-    ('il', ('x', 2, 0), True, 0, 320),
-    ('il', ('x', 2, 0), False, 320, 512),
-    ('mh', 1, 0),
-    ('m1', 1, 1, 0),
     ('m1', 1, 1, 2),
     ('m1', 1, 1, 3),
-    ('m1', 1, 1, 1),
-    ('co', 1, 1),
-    ('tp', 'h', 0, (0, 1)),
-    ('tp', 'h', 0, (2, 3)),
-    ('qx', 2, 0),
-    ('mh', 1, 1),
-    ('il', ('x', 2, 1), True, 0, 320),
-    ('il', ('x', 2, 1), False, 320, 512),
-    ('m1', 1, 2, 0),
     ('m1', 1, 2, 2),
     ('m1', 1, 2, 3),
-    ('m1', 1, 2, 1),
-    ('co', 1, 2),
-    ('ct', 'h', 0, (0, 1)),
-    ('mh', 1, 2),
-    ('qx', 2, 1),
-    ('m1', 1, 3, 0),
     ('m1', 1, 3, 2),
     ('m1', 1, 3, 3),
+    ('il', ('x', 0, 0), True, 0, 256),
+    ('il', ('x', 0, 0), False, 256, 512),
+    ('sl', 0, 0, 512),
+    ('co', 0, 0),
+    ('co', 0, 1),
+    ('il', ('l', 0), True, 0, 256),
+    ('il', ('l', 0), False, 256, 512),
+    ('qx', 0, 0),
+    ('il', ('x', 1, 1), True, 0, 128),
+    ('il', ('x', 1, 1), False, 128, 512),
+    ('ql', 0, 0, 512),
+    ('co', 0, 2),
+    ('co', 0, 3),
+    ('qx', 1, 1),
+    ('il', ('x', 1, 0), True, 0, 256),
+    ('il', ('x', 1, 0), False, 256, 512),
+    ('m1', 0, 0, 0),
+    ('m1', 0, 1, 0),
+    ('m1', 0, 2, 0),
+    ('m1', 1, 0, 1),
+    ('m1', 1, 1, 1),
+    ('m1', 0, 3, 0),
+    ('m1', 1, 2, 1),
     ('m1', 1, 3, 1),
-    ('co', 1, 3),
-    ('ct', 'h', 0, (2, 3)),
-    ('qh', 0, (0, 1)),
-    ('m1', 2, 0, 0),
+    ('mh', 0, 0),
+    ('co', 1, 0),
+    ('mh', 0, 1),
+    ('il', ('x', 2, 1), True, 0, 256),
+    ('mh', 0, 2),
+    ('co', 1, 1),
+    ('mh', 0, 3),
+    ('qx', 1, 0),
+    ('il', ('x', 2, 1), False, 256, 512),
     ('m1', 2, 0, 2),
     ('m1', 2, 0, 3),
-    ('m1', 2, 0, 1),
-    ('co', 2, 0),
-    ('mh', 1, 3),
-    ('qh', 0, (2, 3)),
-    ('il', ('x', 3, 0), True, 0, 256),
-    ('il', ('x', 3, 0), False, 256, 512),
-    ('mh', 2, 0),
-    ('m1', 2, 1, 0),
     ('m1', 2, 1, 2),
     ('m1', 2, 1, 3),
-    ('m1', 2, 1, 1),
-    ('co', 2, 1),
-    ('tp', 'h', 1, (0, 1)),
-    ('tp', 'h', 1, (2, 3)),
-    ('qx', 3, 0),
-    ('mh', 2, 1),
-    ('il', ('x', 3, 1), True, 0, 256),
-    ('il', ('x', 3, 1), False, 256, 512),
-    ('m1', 2, 2, 0),
+    ('tp', 'h', 0, (0, 1)),
+    ('tp', 'h', 0, (2, 3)),
+    ('ct', 'h', 0, (0, 1)),
+    ('ct', 'h', 0, (2, 3)),
+    ('co', 1, 2),
+    ('co', 1, 3),
     ('m1', 2, 2, 2),
     ('m1', 2, 2, 3),
-    ('m1', 2, 2, 1),
-    ('co', 2, 2),
-    ('ct', 'h', 1, (0, 1)),
-    ('mh', 2, 2),
-    ('qx', 3, 1),
-    ('m1', 2, 3, 0),
+    ('il', ('x', 2, 0), True, 0, 256),
+    ('il', ('x', 2, 0), False, 256, 512),
+    ('qx', 2, 1),
+    ('m1', 1, 0, 0),
+    ('m1', 1, 1, 0),
     ('m1', 2, 3, 2),
     ('m1', 2, 3, 3),
-    ('m1', 2, 3, 1),
-    ('co', 2, 3),
-    ('ct', 'h', 1, (2, 3)),
-    ('qh', 1, (0, 1)),
-    ('m1', 3, 0, 0),
+    ('m1', 1, 2, 0),
+    ('m1', 2, 0, 1),
+    ('m1', 2, 1, 1),
+    ('mh', 1, 0),
+    ('co', 2, 0),
+    ('mh', 1, 1),
+    ('il', ('x', 3, 1), True, 0, 256),
     ('m1', 3, 0, 2),
     ('m1', 3, 0, 3),
-    ('m1', 3, 0, 1),
-    ('co', 3, 0),
-    ('mh', 2, 3),
-    ('qh', 1, (2, 3)),
-    ('mh', 3, 0),
-    ('m1', 3, 1, 0),
+    ('mh', 1, 2),
+    ('qx', 2, 0),
+    ('il', ('x', 3, 1), False, 256, 512),
+    ('m1', 1, 3, 0),
+    ('m1', 2, 2, 1),
+    ('m1', 2, 3, 1),
+    ('mh', 1, 3),
+    ('co', 2, 1),
+    ('co', 2, 2),
+    ('co', 2, 3),
+    ('qx', 3, 1),
+    ('il', ('x', 3, 0), True, 0, 256),
+    ('m1', 2, 0, 0),
     ('m1', 3, 1, 2),
     ('m1', 3, 1, 3),
-    ('m1', 3, 1, 1),
-    ('co', 3, 1),
-    ('tp', 'h', 2, (0, 1)),
-    ('tp', 'h', 2, (2, 3)),
-    ('mh', 3, 1),
-    ('m1', 3, 2, 0),
+    ('m1', 2, 1, 0),
     ('m1', 3, 2, 2),
     ('m1', 3, 2, 3),
+    ('mh', 2, 0),
+    ('mh', 2, 1),
+    ('m1', 2, 2, 0),
+    ('m1', 3, 0, 1),
+    ('m1', 2, 3, 0),
+    ('m1', 3, 1, 1),
+    ('co', 3, 0),
+    ('co', 3, 1),
+    ('mh', 2, 2),
+    ('mh', 2, 3),
+    ('il', ('x', 3, 0), False, 256, 512),
+    ('tp', 'h', 1, (0, 1)),
+    ('tp', 'h', 1, (2, 3)),
+    ('tp', 'h', 2, (0, 1)),
+    ('ct', 'h', 1, (0, 1)),
+    ('tp', 'h', 2, (2, 3)),
+    ('ct', 'h', 1, (2, 3)),
+    ('qh', 0, (0, 1)),
+    ('qx', 3, 0),
+    ('qh', 0, (2, 3)),
     ('m1', 3, 2, 1),
-    ('co', 3, 2),
-    ('ct', 'h', 2, (0, 1)),
-    ('mh', 3, 2),
-    ('m1', 3, 3, 0),
     ('m1', 3, 3, 2),
     ('m1', 3, 3, 3),
     ('m1', 3, 3, 1),
+    ('co', 3, 2),
     ('co', 3, 3),
+    ('qh', 1, (0, 1)),
+    ('qh', 1, (2, 3)),
+    ('ct', 'h', 2, (0, 1)),
     ('ct', 'h', 2, (2, 3)),
-    ('qh', 2, (0, 1)),
+    ('m1', 3, 0, 0),
+    ('m1', 3, 1, 0),
+    ('m1', 3, 2, 0),
+    ('mh', 3, 0),
+    ('m2', 0, 0, (0, 1)),
+    ('mh', 3, 1),
+    ('m1', 3, 3, 0),
+    ('mh', 3, 2),
+    ('m2', 0, 1, (0, 1)),
     ('mh', 3, 3),
+    ('qh', 2, (0, 1)),
     ('qh', 2, (2, 3)),
-    ('m2', 0, 0, (0, 1, 2)),
-    ('m2', 0, 1, (0, 1, 2)),
     ('tp', 'h', 3, (0, 1)),
     ('tp', 'h', 3, (2, 3)),
     ('ct', 'h', 3, (0, 1)),
@@ -210,16 +212,16 @@ ORDER = [
     ('qh', 3, (2, 3)),
     ('m2', 0, 2, (0, 1, 2)),
     ('m2', 0, 3, (0, 1, 2)),
-    ('m2', 0, 0, (3,)),
+    ('m2', 0, 0, (2, 3)),
+    ('m2', 0, 1, (2, 3)),
+    ('m2', 0, 2, (3,)),
+    ('m2', 0, 3, (3,)),
     ('my', 0, 0),
     ('cy', 0, 0),
-    ('m2', 0, 1, (3,)),
     ('my', 0, 1),
     ('cy', 0, 1),
-    ('m2', 0, 2, (3,)),
     ('my', 0, 2),
     ('cy', 0, 2),
-    ('m2', 0, 3, (3,)),
     ('my', 0, 3),
     ('cy', 0, 3),
     ('m2', 1, 0, (0, 1, 2, 3)),
@@ -311,9 +313,18 @@ def tile_thc_laplace_mp2_core_product_k6_kernel(
         def ring(pool, tag, depth, shape, dtype):
             turn = turns.get(tag, 0)
             turns[tag] = turn + 1
-            if pool is ps:
-                return pool.tile(shape, dtype, name="%s_%d" % (tag, turn), tag="%s%d" % (tag, turn % depth))
             return pool.tile(shape, dtype, name="%s_%d" % (tag, turn), tag="%s%d" % (tag, turn % depth), align_bytes=64)
+
+        free_banks = list(range(BANKS))
+        bank_of = {}
+
+        def take_bank(key):
+            bank_of[key] = free_banks.pop(0)
+            turns["bank"] = turns.get("bank", 0) + 1
+            return ps.tile([P, W], F32, name="bank_%d" % turns["bank"], tag="bank%d" % bank_of[key])
+
+        def give_bank(key):
+            free_banks.append(bank_of[key])
 
         def keep(name, shape, dtype):
             return sb.tile(shape, dtype, name=name, align_bytes=64)
@@ -324,11 +335,9 @@ def tile_thc_laplace_mp2_core_product_k6_kernel(
         ident = keep("ident", [P, P], F32)
         make_identity(nc, ident[:])
 
-        xf_sc0 = keep("xf_sc0", [P, 2, W], U8)
-        xf_sc1 = keep("xf_sc1", [P, 2, (NCH - 1) * W], U8)
+        xf_sc = keep("xf_sc", [P, NCH, 2, W], U8)
         c_sc = keep("c_sc", [P, NCH * W], U8)
-        nc.vector.memset(xf_sc0[:].rearrange("p g n -> p (g n)").bitcast(U32), 0)
-        nc.vector.memset(xf_sc1[:].rearrange("p g n -> p (g n)").bitcast(U32), 0)
+        nc.vector.memset(xf_sc[:].rearrange("p g k n -> p (g k n)").bitcast(U32), 0)
         nc.vector.memset(c_sc[:].bitcast(U32), 0)
 
         eo_sb = keep("eo_sb", [P, PACK], BF16)
@@ -365,15 +374,12 @@ def tile_thc_laplace_mp2_core_product_k6_kernel(
             src = c_words.rearrange("g p n t -> p g (n t)")[:, :, PACK * W * n : PACK * W * (n + 1)]
             nc.sync.dma_start(out=c_w[n][:].bitcast(I32), in_=src.bitcast(I32))
 
-        def load_xf_scales(plane, cols):
+        def load_xs(g):
             for q in range(QUADS):
                 nc.sync.dma_start(
-                    out=plane[32 * q : 32 * q + 4, :, :].bitcast(I32),
-                    in_=xf_scales[:, 4 * q : 4 * q + 4, cols].rearrange("k r n -> r k n").bitcast(I32),
+                    out=xf_sc[32 * q : 32 * q + 4, g, :, :].bitcast(I32),
+                    in_=xf_scales[:, 4 * q : 4 * q + 4, chunk(g)].rearrange("k r n -> r k n").bitcast(I32),
                 )
-
-        def load_xs(i):
-            load_xf_scales(*[(xf_sc0, slice(0, W)), (xf_sc1, slice(W, NCH * W))][i])
 
         def load_cs():
             for q in range(QUADS):
@@ -432,15 +438,15 @@ def tile_thc_laplace_mp2_core_product_k6_kernel(
 
         def mm1(g, b, k):
             if k == 0:
-                o_ps[g, b] = ring(ps, "acc", ACC_BANKS, [P, W], F32)
+                o_ps[g, b] = take_bank(("o", g, b))
             if k > 0:
                 v_done[g, b] = v_done.get((g, b), 0) + 1
             if k > 0 and v_done[g, b] == 1:
-                v_ps[g, b] = ring(ps, "acc", ACC_BANKS, [P, W], F32)
+                v_ps[g, b] = take_bank(("v", g, b))
             if k < 2:
                 rhs, rhs_scale = x_codes[:, g, k, :].bitcast(FP8X4), x_sc[:, g, k, :]
             else:
-                rhs, rhs_scale = xf_w[g][:, k - 2, :].bitcast(FP4X4), (xf_sc1[:, k - 2, chunk(g - 1)] if g else xf_sc0[:, k - 2, :])
+                rhs, rhs_scale = xf_w[g][:, k - 2, :].bitcast(FP4X4), xf_sc[:, g, k - 2, :]
             nc.tensor.matmul_mx(
                 out=(o_ps if k == 0 else v_ps)[g, b][:],
                 lhsT=l_codes[:, k, rows(b)].bitcast(FP8X4), lhsT_scale=l_sc[:, k, rows(b)],
@@ -459,16 +465,18 @@ def tile_thc_laplace_mp2_core_product_k6_kernel(
 
         def copy_o(g, b):
             o_sb[g, b] = ring(sb, "o_sb", 6, [P, W], F32)
-            nc.scalar.copy(out=as_pairs(o_sb[g, b][:]), in_=by_pairs(o_ps[g, b][:]))
+            nc.scalar.copy(out=as_pairs(o_sb[g, b][:]), in_=by_pairs((v_ps if COPY_V else o_ps)[g, b][:]))
+            give_bank(("v" if COPY_V else "o", g, b))
 
         def mul_h(g, b):
-            paired["h", g, b] = ring(sb, "paired", 8, [P, W], BF16)
+            paired["h", g, b] = ring(sb, "paired", 12, [P, W], BF16)
             nc.vector.tensor_tensor(
-                out=as_pairs(paired["h", g, b][:]), in0=by_pairs(v_ps[g, b][:]), in1=as_pairs(o_sb[g, b][:]), op=MULT,
+                out=as_pairs(paired["h", g, b][:]), in0=by_pairs((o_ps if COPY_V else v_ps)[g, b][:]), in1=as_pairs(o_sb[g, b][:]), op=MULT,
             )
+            give_bank(("o" if COPY_V else "v", g, b))
 
         def turn(kind, c, bs):
-            bank = ring(ps, "tp", TP_BANKS, [P, 4, P], F32)
+            bank = take_bank((kind, c, bs))[:].rearrange("p (z r) -> p z r", z=4)
             for i, b in enumerate(bs):
                 words = paired[kind, c, b][:].bitcast(F32)
                 for u in range(2):
@@ -477,13 +485,14 @@ def tile_thc_laplace_mp2_core_product_k6_kernel(
 
         def copy_turned(kind, c, bs):
             bank = turned[kind, c, bs]
-            dst = ring(sb, "kfirst", 4, [P, 2 * W], BF16)
+            dst = ring(sb, "kfirst", 6, [P, 2 * W], BF16)
             nb = len(bs)
             nc.scalar.copy(
                 out=dst[:, 0 : nb * W].bitcast(F32).rearrange("p (i r u) -> p i r u", i=nb, u=2),
                 in_=bank[:, 0 : 2 * nb, :].rearrange("p (i u) r -> p i r u", u=2),
             )
             turned[kind, c, bs] = dst
+            give_bank((kind, c, bs))
 
         def quant_h(g, bs):
             cols = slice(bs[0] * P, (bs[-1] + 1) * P)
@@ -494,7 +503,7 @@ def tile_thc_laplace_mp2_core_product_k6_kernel(
         def mm2(n, b, gs):
             for g in gs:
                 if g == 0:
-                    y_ps[n, b] = ring(ps, "acc", ACC_BANKS, [P, W], F32)
+                    y_ps[n, b] = take_bank(("y", n, b))
                 nc.tensor.matmul_mx(
                     out=y_ps[n, b][:],
                     lhsT=h_codes[:, g, rows(b)].bitcast(FP8X4), lhsT_scale=h_sc[:, g, rows(b)],
@@ -505,10 +514,11 @@ def tile_thc_laplace_mp2_core_product_k6_kernel(
         def mul_y(n, b):
             y_sb[n, b] = ring(sb, "y_sb", 8, [P, W], F32)
             nc.vector.tensor_tensor(out=y_sb[n, b][:], in0=y_ps[n, b][:], in1=w_sb[:, chunk(n)], op=MULT)
+            give_bank(("y", n, b))
             nc.sync.dma_start(out=out_0[rows(b), chunk(n)], in_=y_sb[n, b][:])
 
         def cast_y(n, b):
-            paired["y", n, b] = ring(sb, "paired", 8, [P, W], BF16)
+            paired["y", n, b] = ring(sb, "paired", 12, [P, W], BF16)
             nc.scalar.copy(out=as_pairs(paired["y", n, b][:]), in_=by_pairs(y_sb[n, b][:]))
 
         def quant_y(n, bs):
@@ -523,7 +533,7 @@ def tile_thc_laplace_mp2_core_product_k6_kernel(
             nc.sync.dma_start(out=dst[:, cols], in_=y_codes[n][:, cols].bitcast(I32))
 
         def mul_y_bf16(n, b):
-            paired["y", n, b] = ring(sb, "paired", 8, [P, W], BF16)
+            paired["y", n, b] = ring(sb, "paired", 12, [P, W], BF16)
             nc.vector.tensor_tensor(
                 out=as_pairs(paired["y", n, b][:]), in0=by_pairs(y_ps[n, b][:]), in1=by_pairs(w_sb[:, chunk(n)]), op=MULT,
             )

@@ -20,6 +20,7 @@ NCH = 4
 NB = 4
 QUADS = 4
 BANKS = 8
+NBLK = 2
 COPY_V = True
 ORDER = [
     ('ll', 2),
@@ -168,28 +169,26 @@ ORDER = [
     ('m1', 3, 0, 1),
     ('m1', 2, 3, 0),
     ('m1', 3, 1, 1),
-    ('co', 3, 0),
-    ('co', 3, 1),
     ('mh', 2, 2),
+    ('co', 3, 0),
     ('mh', 2, 3),
+    ('co', 3, 1),
     ('il', ('x', 3, 0), False, 256, 512),
     ('tp', 'h', 1, (0, 1)),
     ('tp', 'h', 1, (2, 3)),
-    ('tp', 'h', 2, (0, 1)),
     ('ct', 'h', 1, (0, 1)),
+    ('tp', 'h', 2, (0, 1)),
     ('tp', 'h', 2, (2, 3)),
     ('ct', 'h', 1, (2, 3)),
-    ('qh', 0, (0, 1)),
+    ('qh', 0, 0, 512),
     ('qx', 3, 0),
-    ('qh', 0, (2, 3)),
     ('m1', 3, 2, 1),
     ('m1', 3, 3, 2),
     ('m1', 3, 3, 3),
     ('m1', 3, 3, 1),
     ('co', 3, 2),
     ('co', 3, 3),
-    ('qh', 1, (0, 1)),
-    ('qh', 1, (2, 3)),
+    ('qh', 1, 0, 512),
     ('ct', 'h', 2, (0, 1)),
     ('ct', 'h', 2, (2, 3)),
     ('m1', 3, 0, 0),
@@ -202,96 +201,104 @@ ORDER = [
     ('mh', 3, 2),
     ('m2', 0, 1, (0, 1)),
     ('mh', 3, 3),
-    ('qh', 2, (0, 1)),
-    ('qh', 2, (2, 3)),
+    ('qh', 2, 0, 512),
+    ('m2', 0, 2, (0, 1)),
     ('tp', 'h', 3, (0, 1)),
     ('tp', 'h', 3, (2, 3)),
     ('ct', 'h', 3, (0, 1)),
     ('ct', 'h', 3, (2, 3)),
-    ('qh', 3, (0, 1)),
-    ('qh', 3, (2, 3)),
-    ('m2', 0, 2, (0, 1, 2)),
+    ('qh', 3, 0, 512),
     ('m2', 0, 3, (0, 1, 2)),
-    ('m2', 0, 0, (2, 3)),
-    ('m2', 0, 1, (2, 3)),
-    ('m2', 0, 2, (3,)),
-    ('m2', 0, 3, (3,)),
+    ('m2', 0, 2, (2,)),
+    ('m2', 0, 0, (2,)),
+    ('m2', 0, 1, (2,)),
+    ('m2', 0, 0, (3,)),
     ('my', 0, 0),
     ('cy', 0, 0),
+    ('m2', 0, 1, (3,)),
     ('my', 0, 1),
     ('cy', 0, 1),
+    ('m2', 0, 2, (3,)),
     ('my', 0, 2),
     ('cy', 0, 2),
+    ('m2', 0, 3, (3,)),
     ('my', 0, 3),
     ('cy', 0, 3),
     ('m2', 1, 0, (0, 1, 2, 3)),
-    ('m2', 1, 1, (0, 1, 2, 3)),
-    ('tp', 'y', 0, (0, 1)),
-    ('tp', 'y', 0, (2, 3)),
+    ('tb', 0, 0),
+    ('tb', 0, 1),
     ('my', 1, 0),
-    ('ct', 'y', 0, (0, 1)),
-    ('ct', 'y', 0, (2, 3)),
     ('cy', 1, 0),
+    ('m2', 1, 1, (0, 1, 2, 3)),
+    ('tb', 0, 2),
+    ('tb', 0, 3),
+    ('gb', 0, 0),
     ('my', 1, 1),
+    ('gb', 0, 1),
     ('cy', 1, 1),
-    ('qy', 0, (0, 1)),
     ('m2', 1, 2, (0, 1, 2, 3)),
     ('my', 1, 2),
-    ('qy', 0, (2, 3)),
-    ('sw', 0, 0, 512),
     ('cy', 1, 2),
+    ('qb', 0, 0),
+    ('qb', 0, 1),
+    ('qb', 0, 2),
+    ('qb', 0, 3),
+    ('sb', 0),
     ('m2', 1, 3, (0, 1, 2, 3)),
     ('my', 1, 3),
     ('cy', 1, 3),
     ('m2', 2, 0, (0, 1, 2, 3)),
-    ('m2', 2, 1, (0, 1, 2, 3)),
-    ('tp', 'y', 1, (0, 1)),
-    ('tp', 'y', 1, (2, 3)),
+    ('tb', 1, 0),
+    ('tb', 1, 1),
     ('my', 2, 0),
-    ('ct', 'y', 1, (0, 1)),
-    ('ct', 'y', 1, (2, 3)),
     ('cy', 2, 0),
+    ('m2', 2, 1, (0, 1, 2, 3)),
+    ('tb', 1, 2),
+    ('tb', 1, 3),
+    ('gb', 1, 0),
     ('my', 2, 1),
+    ('gb', 1, 1),
     ('cy', 2, 1),
-    ('qy', 1, (0, 1)),
     ('m2', 2, 2, (0, 1, 2, 3)),
     ('my', 2, 2),
-    ('qy', 1, (2, 3)),
-    ('sw', 1, 0, 512),
     ('cy', 2, 2),
+    ('qb', 1, 0),
+    ('qb', 1, 1),
+    ('qb', 1, 2),
+    ('qb', 1, 3),
+    ('sb', 1),
     ('m2', 2, 3, (0, 1, 2, 3)),
     ('my', 2, 3),
     ('cy', 2, 3),
+    ('sbs',),
     ('m2', 3, 0, (0, 1, 2, 3)),
-    ('m2', 3, 1, (0, 1, 2, 3)),
-    ('tp', 'y', 2, (0, 1)),
-    ('tp', 'y', 2, (2, 3)),
     ('my', 3, 0),
-    ('ct', 'y', 2, (0, 1)),
-    ('ct', 'y', 2, (2, 3)),
     ('cy', 3, 0),
+    ('m2', 3, 1, (0, 1, 2, 3)),
     ('my', 3, 1),
     ('cy', 3, 1),
-    ('qy', 2, (0, 1)),
+    ('tp', 'y', 2, (0, 1)),
+    ('tp', 'y', 2, (2, 3)),
+    ('cz', 2, (0, 1), 0, 0, 128, True),
+    ('cz', 2, (2, 3), 0, 0, 128, True),
     ('m2', 3, 2, (0, 1, 2, 3)),
     ('my', 3, 2),
-    ('qy', 2, (2, 3)),
-    ('sw', 2, 0, 512),
     ('cy', 3, 2),
+    ('qy', 2, 0, 512),
+    ('sw', 2, 0, 512),
     ('m2', 3, 3, (0, 1, 2, 3)),
     ('tp', 'y', 3, (0, 1)),
-    ('tp', 'y', 3, (2,)),
-    ('ct', 'y', 3, (0, 1)),
+    ('cz', 3, (0, 1), 0, 0, 128, True),
     ('mb', 3, 3),
     ('my', 3, 3),
-    ('ct', 'y', 3, (2,)),
-    ('tp', 'y', 3, (3,)),
-    ('qy', 3, (0, 1)),
-    ('ct', 'y', 3, (3,)),
-    ('qy', 3, (2,)),
-    ('sw', 3, 0, 384),
-    ('qy', 3, (3,)),
-    ('sw', 3, 384, 512),
+    ('tp', 'y', 3, (2, 3), 0),
+    ('tp', 'y', 3, (2, 3), 1),
+    ('cz', 3, (2, 3), 0, 0, 64, True),
+    ('cz', 3, (2, 3), 1, 64, 128, False),
+    ('qy', 3, 0, 256),
+    ('sw', 3, 0, 256),
+    ('qy', 3, 256, 512),
+    ('sw', 3, 256, 512),
     ('ss',),
 ]
 
@@ -343,13 +350,13 @@ def tile_thc_laplace_mp2_core_product_k6_kernel(
         eo_sb = keep("eo_sb", [P, PACK], BF16)
         ev_sb = keep("ev_sb", [P, PACK], BF16)
         ef_sb = keep("ef_sb", [P, 2, PACK], BF16)
-        nc.scalar.dma_start(out=eo_sb[:], in_=eo.rearrange("(p j) -> p j", j=PACK))
-        nc.scalar.dma_start(out=ev_sb[:], in_=ev.rearrange("(p j) -> p j", j=PACK))
         nc.scalar.dma_start(out=ef_sb[:], in_=ef.rearrange("(g p j) -> p g j", g=2, j=PACK))
+        nc.scalar.dma_start(out=ev_sb[:], in_=ev.rearrange("(p j) -> p j", j=PACK))
+        nc.scalar.dma_start(out=eo_sb[:], in_=eo.rearrange("(p j) -> p j", j=PACK))
         damp = keep("damp", [P, 4 * PACK], F32)
-        nc.scalar.activation(out=damp[:, 0:4], in_=eo_sb[:], func=EXP, scale=-1.0)
-        nc.scalar.activation(out=damp[:, 4:8], in_=ev_sb[:], func=EXP, scale=-1.0)
         nc.scalar.activation(out=damp[:, 8:16], in_=ef_sb[:].rearrange("p g j -> p (g j)"), func=EXP, scale=-1.0)
+        nc.scalar.activation(out=damp[:, 4:8], in_=ev_sb[:], func=EXP, scale=-1.0)
+        nc.scalar.activation(out=damp[:, 0:4], in_=eo_sb[:], func=EXP, scale=-1.0)
 
         l_src = [xo_b, xv_b, xf_b[0:W, :], xf_b[W : 2 * W, :]]
         x_src = [xo_g, xv_g]
@@ -400,6 +407,7 @@ def tile_thc_laplace_mp2_core_product_k6_kernel(
         h_codes = keep("h_codes", [P, NCH, W], U32)
         h_sc = keep("h_sc", [P, NCH, W], U8)
         y_sc = keep("y_sc", [P, W], U8)
+        yb_sc = keep("yb_sc", [P, NBLK, P], U8)
 
         def scale_l(k, c0, c1):
             if ("l", k) not in src_of:
@@ -469,34 +477,59 @@ def tile_thc_laplace_mp2_core_product_k6_kernel(
             give_bank(("v" if COPY_V else "o", g, b))
 
         def mul_h(g, b):
-            paired["h", g, b] = ring(sb, "paired", 12, [P, W], BF16)
+            paired["h", g, b] = ring(sb, "paired", 10, [P, W], BF16)
             nc.vector.tensor_tensor(
                 out=as_pairs(paired["h", g, b][:]), in0=by_pairs((o_ps if COPY_V else v_ps)[g, b][:]), in1=as_pairs(o_sb[g, b][:]), op=MULT,
             )
             give_bank(("o" if COPY_V else "v", g, b))
 
-        def turn(kind, c, bs):
-            bank = take_bank((kind, c, bs))[:].rearrange("p (z r) -> p z r", z=4)
+        def turn(kind, c, bs, copy=0):
+            key = (kind, c, bs, copy)
+            bank = take_bank(key)
             for i, b in enumerate(bs):
                 words = paired[kind, c, b][:].bitcast(F32)
                 for u in range(2):
-                    nc.tensor.transpose(bank[:, 2 * i + u, :], words[:, u * P : (u + 1) * P], ident[:])
-            turned[kind, c, bs] = bank
+                    slot = 2 * u + i if kind == "h" else 2 * i + u
+                    nc.tensor.transpose(bank[:, slot * P : (slot + 1) * P], words[:, u * P : (u + 1) * P], ident[:])
+            turned[key] = bank
 
-        def copy_turned(kind, c, bs):
-            bank = turned[kind, c, bs]
-            dst = ring(sb, "kfirst", 6, [P, 2 * W], BF16)
-            nb = len(bs)
-            nc.scalar.copy(
-                out=dst[:, 0 : nb * W].bitcast(F32).rearrange("p (i r u) -> p i r u", i=nb, u=2),
-                in_=bank[:, 0 : 2 * nb, :].rearrange("p (i u) r -> p i r u", u=2),
-            )
-            turned[kind, c, bs] = dst
-            give_bank((kind, c, bs))
+        kfirst = {}
 
-        def quant_h(g, bs):
-            cols = slice(bs[0] * P, (bs[-1] + 1) * P)
-            quantize(h_codes[:, g, cols], h_sc[:, g, cols], turned["h", g, bs][:, 0 : len(bs) * W])
+        def copy_h(kind, g, bs):
+            if ("h", g) not in kfirst:
+                kfirst["h", g] = ring(sb, "kfirst", 3, [P, W * PACK], BF16)
+            dst = kfirst["h", g][:].bitcast(F32).rearrange("p (z a u) -> p z a u", z=4, u=2)
+            src = turned["h", g, bs, 0][:].rearrange("p (u a z) -> p z a u", u=2, z=4)
+            nc.scalar.copy(out=dst[:, :, 32 * bs[0] : 32 * bs[0] + 64, :], in_=src)
+            give_bank(("h", g, bs, 0))
+
+        def quant_h(g, c0, c1):
+            quantize(h_codes[:, g, c0:c1], h_sc[:, g, c0:c1], kfirst["h", g][:, PACK * c0 : PACK * c1])
+
+        def copy_y(n, bs, copy, a0, a1, on_scalar):
+            if ("y", n) not in kfirst:
+                kfirst["y", n] = ring(sb, "kfirst", 3, [P, W * PACK], BF16)
+            dst = kfirst["y", n][:].bitcast(F32).rearrange("p (a r) -> p a r", r=8)[:, a0:a1, 2 * bs[0] : 2 * bs[0] + 4]
+            src = turned["y", n, bs, copy][:].rearrange("p (r a) -> p a r", r=4)[:, a0:a1, :]
+            if on_scalar:
+                nc.scalar.copy(out=dst, in_=src)
+            else:
+                nc.vector.tensor_copy(out=dst, in_=src)
+            give_bank(("y", n, bs, copy))
+
+        blocks = {}
+
+        def turn_blocks(n, b):
+            if n not in blocks:
+                blocks[n] = ring(sb, "damped", 3, [P, NB * 2 * P], F32)
+            nc.vector.transpose(out=blocks[n][:, 2 * P * b : 2 * P * (b + 1)], in_=paired["y", n, b][:].bitcast(F32))
+
+        def gather_blocks(n, h):
+            if ("y", n) not in kfirst:
+                kfirst["y", n] = ring(sb, "kfirst", 3, [P, W * PACK], BF16)
+            dst = kfirst["y", n][:].bitcast(F32).rearrange("p (c i r) -> p c r i", i=4, r=8)
+            src = blocks[n][:].rearrange("p (r c i) -> p c r i", r=8, i=4)
+            nc.scalar.copy(out=dst[:, 16 * h : 16 * h + 16, :, :], in_=src[:, 16 * h : 16 * h + 16, :, :])
 
         y_codes = {}
 
@@ -512,28 +545,43 @@ def tile_thc_laplace_mp2_core_product_k6_kernel(
                 )
 
         def mul_y(n, b):
-            y_sb[n, b] = ring(sb, "y_sb", 8, [P, W], F32)
+            y_sb[n, b] = ring(sb, "y_sb", 7, [P, W], F32)
             nc.vector.tensor_tensor(out=y_sb[n, b][:], in0=y_ps[n, b][:], in1=w_sb[:, chunk(n)], op=MULT)
             give_bank(("y", n, b))
-            nc.sync.dma_start(out=out_0[rows(b), chunk(n)], in_=y_sb[n, b][:])
+            nc.sync.dma_start(out=out_0.rearrange("(p z) n -> z p n", z=NB)[b][:, chunk(n)], in_=y_sb[n, b][:])
 
         def cast_y(n, b):
-            paired["y", n, b] = ring(sb, "paired", 12, [P, W], BF16)
+            paired["y", n, b] = ring(sb, "paired", 10, [P, W], BF16)
             nc.scalar.copy(out=as_pairs(paired["y", n, b][:]), in_=by_pairs(y_sb[n, b][:]))
 
-        def quant_y(n, bs):
+        def quant_y(n, c0, c1):
             if n not in y_codes:
                 y_codes[n] = keep("y_codes%d" % n, [P, W], U32)
-            cols = slice(bs[0] * P, (bs[-1] + 1) * P)
-            quantize(y_codes[n][:, cols], y_sc[4 * n :, cols], turned["y", n, bs][:, 0 : len(bs) * W])
+            quantize(y_codes[n][:, c0:c1], y_sc[4 * (n - NBLK) :, c0:c1], kfirst["y", n][:, PACK * c0 : PACK * c1])
+
+        def quant_blocks(n, mh):
+            if n not in y_codes:
+                y_codes[n] = keep("y_codes%d" % n, [P, W], U32)
+            cols = slice(mh * P, (mh + 1) * P)
+            quantize(y_codes[n][:, cols], yb_sc[4 * mh :, n, :], kfirst["y", n][:, mh * W : (mh + 1) * W])
 
         def store_words(n, c0, c1):
-            cols = slice(c0, c1)
             dst = out_1[n].rearrange("p m t -> p (m t)").bitcast(I32)
-            nc.sync.dma_start(out=dst[:, cols], in_=y_codes[n][:, cols].bitcast(I32))
+            nc.sync.dma_start(out=dst[:, c0:c1], in_=y_codes[n][:, c0:c1].bitcast(I32))
+
+        def store_block_words(n):
+            dst = out_1[n].rearrange("p m t -> p (m t)").bitcast(I32).rearrange("(h l) b -> l h b", l=32)
+            for q in range(QUADS):
+                src = y_codes[n][32 * q : 32 * q + 32, :].bitcast(I32).rearrange("l (h b) -> l h b", b=P)
+                nc.sync.dma_start(out=dst[:, :, q * P : (q + 1) * P], in_=src)
+
+        def store_block_scales():
+            for q in range(QUADS):
+                dst = out_2[0:NBLK, :, q * P : (q + 1) * P].rearrange("n r b -> r n b")
+                nc.sync.dma_start(out=dst.bitcast(I32), in_=yb_sc[32 * q : 32 * q + 16, :, :].bitcast(I32))
 
         def mul_y_bf16(n, b):
-            paired["y", n, b] = ring(sb, "paired", 12, [P, W], BF16)
+            paired["y", n, b] = ring(sb, "paired", 10, [P, W], BF16)
             nc.vector.tensor_tensor(
                 out=as_pairs(paired["y", n, b][:]), in0=by_pairs(y_ps[n, b][:]), in1=by_pairs(w_sb[:, chunk(n)]), op=MULT,
             )
@@ -542,13 +590,13 @@ def tile_thc_laplace_mp2_core_product_k6_kernel(
             for q in range(QUADS):
                 eng = nc.sync if q % 2 else nc.scalar
                 eng.dma_start(
-                    out=out_2[:, 4 * q : 4 * q + 4, :].bitcast(I32),
-                    in_=y_sc[32 * q : 32 * q + 16, :].bitcast(I32),
+                    out=out_2[NBLK:NCH, 4 * q : 4 * q + 4, :].bitcast(I32),
+                    in_=y_sc[32 * q : 32 * q + 4 * (NCH - NBLK), :].bitcast(I32),
                 )
 
         steps = {
             "sl": scale_l, "il": interleave, "ql": quant_l, "qx": quant_x, "m1": mm1, "co": copy_o, "mh": mul_h,
-            "tp": turn, "ct": copy_turned, "qh": quant_h, "m2": mm2, "my": mul_y, "cy": cast_y, "qy": quant_y,
+            "tp": turn, "ct": copy_h, "cz": copy_y, "tb": turn_blocks, "gb": gather_blocks, "qb": quant_blocks, "sb": store_block_words, "sbs": store_block_scales, "qh": quant_h, "m2": mm2, "my": mul_y, "cy": cast_y, "qy": quant_y,
             "lx": load_x, "ll": load_l, "lf": load_xf, "lc": load_c, "ls": load_xs, "lcs": load_cs, "lw": load_w,
             "sw": store_words, "mb": mul_y_bf16, "ss": store_scales,
         }

@@ -16,291 +16,28 @@ EXP = mybir.ActivationFunctionType.Exp
 P = 128
 PACK = 4
 W = 512
-NCH = 4
-NB = 4
+CHUNKS = 4
+TILES = 4
 QUADS = 4
 BANKS = 8
-NBLK = 2
-COPY_V = True
-ORDER = [
-    ('ll', 2),
-    ('ll', 3),
-    ('ll', 1),
-    ('ls', 0),
-    ('lf', 0),
-    ('lx', 0, 1),
-    ('lx', 0, 0),
-    ('ll', 0),
-    ('ls', 1),
-    ('lf', 1),
-    ('lx', 1, 1),
-    ('lx', 1, 0),
-    ('ls', 2),
-    ('lf', 2),
-    ('lx', 2, 1),
-    ('lx', 2, 0),
-    ('ls', 3),
-    ('lf', 3),
-    ('lx', 3, 1),
-    ('lx', 3, 0),
-    ('lcs',),
-    ('lc', 0),
-    ('lw',),
-    ('lc', 1),
-    ('lc', 2),
-    ('lc', 3),
-    ('sl', 2, 0, 512),
-    ('il', ('l', 2), True, 0, 256),
-    ('il', ('l', 2), False, 256, 512),
-    ('sl', 3, 0, 512),
-    ('il', ('l', 3), True, 0, 256),
-    ('ql', 2, 0, 512),
-    ('m1', 0, 0, 2),
-    ('m1', 0, 1, 2),
-    ('m1', 0, 2, 2),
-    ('m1', 0, 3, 2),
-    ('sl', 1, 0, 512),
-    ('il', ('l', 1), True, 0, 256),
-    ('il', ('l', 3), False, 256, 512),
-    ('il', ('l', 1), False, 256, 512),
-    ('ql', 3, 0, 512),
-    ('m1', 0, 0, 3),
-    ('m1', 0, 1, 3),
-    ('m1', 0, 2, 3),
-    ('m1', 0, 3, 3),
-    ('il', ('x', 0, 1), True, 0, 256),
-    ('il', ('x', 0, 1), False, 256, 512),
-    ('ql', 1, 0, 512),
-    ('qx', 0, 1),
-    ('m1', 0, 0, 1),
-    ('m1', 0, 1, 1),
-    ('m1', 0, 2, 1),
-    ('m1', 0, 3, 1),
-    ('m1', 1, 0, 2),
-    ('m1', 1, 0, 3),
-    ('m1', 1, 1, 2),
-    ('m1', 1, 1, 3),
-    ('m1', 1, 2, 2),
-    ('m1', 1, 2, 3),
-    ('m1', 1, 3, 2),
-    ('m1', 1, 3, 3),
-    ('il', ('x', 0, 0), True, 0, 256),
-    ('il', ('x', 0, 0), False, 256, 512),
-    ('sl', 0, 0, 512),
-    ('co', 0, 0),
-    ('co', 0, 1),
-    ('il', ('l', 0), True, 0, 256),
-    ('il', ('l', 0), False, 256, 512),
-    ('qx', 0, 0),
-    ('il', ('x', 1, 1), True, 0, 128),
-    ('il', ('x', 1, 1), False, 128, 512),
-    ('ql', 0, 0, 512),
-    ('co', 0, 2),
-    ('co', 0, 3),
-    ('qx', 1, 1),
-    ('il', ('x', 1, 0), True, 0, 256),
-    ('il', ('x', 1, 0), False, 256, 512),
-    ('m1', 0, 0, 0),
-    ('m1', 0, 1, 0),
-    ('m1', 0, 2, 0),
-    ('m1', 1, 0, 1),
-    ('m1', 1, 1, 1),
-    ('m1', 0, 3, 0),
-    ('m1', 1, 2, 1),
-    ('m1', 1, 3, 1),
-    ('mh', 0, 0),
-    ('co', 1, 0),
-    ('mh', 0, 1),
-    ('il', ('x', 2, 1), True, 0, 256),
-    ('mh', 0, 2),
-    ('co', 1, 1),
-    ('mh', 0, 3),
-    ('qx', 1, 0),
-    ('il', ('x', 2, 1), False, 256, 512),
-    ('m1', 2, 0, 2),
-    ('m1', 2, 0, 3),
-    ('m1', 2, 1, 2),
-    ('m1', 2, 1, 3),
-    ('tp', 'h', 0, (0, 1)),
-    ('tp', 'h', 0, (2, 3)),
-    ('ct', 'h', 0, (0, 1)),
-    ('ct', 'h', 0, (2, 3)),
-    ('co', 1, 2),
-    ('co', 1, 3),
-    ('m1', 2, 2, 2),
-    ('m1', 2, 2, 3),
-    ('il', ('x', 2, 0), True, 0, 256),
-    ('il', ('x', 2, 0), False, 256, 512),
-    ('qx', 2, 1),
-    ('m1', 1, 0, 0),
-    ('m1', 1, 1, 0),
-    ('m1', 2, 3, 2),
-    ('m1', 2, 3, 3),
-    ('m1', 1, 2, 0),
-    ('m1', 2, 0, 1),
-    ('m1', 2, 1, 1),
-    ('mh', 1, 0),
-    ('co', 2, 0),
-    ('mh', 1, 1),
-    ('il', ('x', 3, 1), True, 0, 256),
-    ('m1', 3, 0, 2),
-    ('m1', 3, 0, 3),
-    ('mh', 1, 2),
-    ('qx', 2, 0),
-    ('il', ('x', 3, 1), False, 256, 512),
-    ('m1', 1, 3, 0),
-    ('m1', 2, 2, 1),
-    ('m1', 2, 3, 1),
-    ('mh', 1, 3),
-    ('co', 2, 1),
-    ('co', 2, 2),
-    ('co', 2, 3),
-    ('qx', 3, 1),
-    ('il', ('x', 3, 0), True, 0, 256),
-    ('m1', 2, 0, 0),
-    ('m1', 3, 1, 2),
-    ('m1', 3, 1, 3),
-    ('m1', 2, 1, 0),
-    ('m1', 3, 2, 2),
-    ('m1', 3, 2, 3),
-    ('mh', 2, 0),
-    ('mh', 2, 1),
-    ('m1', 2, 2, 0),
-    ('m1', 3, 0, 1),
-    ('m1', 2, 3, 0),
-    ('m1', 3, 1, 1),
-    ('mh', 2, 2),
-    ('co', 3, 0),
-    ('mh', 2, 3),
-    ('co', 3, 1),
-    ('il', ('x', 3, 0), False, 256, 512),
-    ('tp', 'h', 1, (0, 1)),
-    ('tp', 'h', 1, (2, 3)),
-    ('ct', 'h', 1, (0, 1)),
-    ('tp', 'h', 2, (0, 1)),
-    ('tp', 'h', 2, (2, 3)),
-    ('ct', 'h', 1, (2, 3)),
-    ('qh', 0, 0, 512),
-    ('qx', 3, 0),
-    ('m1', 3, 2, 1),
-    ('m1', 3, 3, 2),
-    ('m1', 3, 3, 3),
-    ('m1', 3, 3, 1),
-    ('co', 3, 2),
-    ('co', 3, 3),
-    ('qh', 1, 0, 512),
-    ('ct', 'h', 2, (0, 1)),
-    ('ct', 'h', 2, (2, 3)),
-    ('m1', 3, 0, 0),
-    ('m1', 3, 1, 0),
-    ('m1', 3, 2, 0),
-    ('mh', 3, 0),
-    ('m2', 0, 0, (0, 1)),
-    ('mh', 3, 1),
-    ('m1', 3, 3, 0),
-    ('mh', 3, 2),
-    ('m2', 0, 1, (0, 1)),
-    ('mh', 3, 3),
-    ('qh', 2, 0, 512),
-    ('m2', 0, 2, (0, 1)),
-    ('tp', 'h', 3, (0, 1)),
-    ('tp', 'h', 3, (2, 3)),
-    ('ct', 'h', 3, (0, 1)),
-    ('ct', 'h', 3, (2, 3)),
-    ('qh', 3, 0, 512),
-    ('m2', 0, 3, (0, 1, 2)),
-    ('m2', 0, 2, (2,)),
-    ('m2', 0, 0, (2,)),
-    ('m2', 0, 1, (2,)),
-    ('m2', 0, 0, (3,)),
-    ('my', 0, 0),
-    ('cy', 0, 0),
-    ('m2', 0, 1, (3,)),
-    ('my', 0, 1),
-    ('cy', 0, 1),
-    ('m2', 0, 2, (3,)),
-    ('my', 0, 2),
-    ('cy', 0, 2),
-    ('m2', 0, 3, (3,)),
-    ('my', 0, 3),
-    ('cy', 0, 3),
-    ('m2', 1, 0, (0, 1, 2, 3)),
-    ('tb', 0, 0),
-    ('tb', 0, 1),
-    ('my', 1, 0),
-    ('cy', 1, 0),
-    ('m2', 1, 1, (0, 1, 2, 3)),
-    ('tb', 0, 2),
-    ('tb', 0, 3),
-    ('gb', 0, 0),
-    ('my', 1, 1),
-    ('gb', 0, 1),
-    ('cy', 1, 1),
-    ('m2', 1, 2, (0, 1, 2, 3)),
-    ('my', 1, 2),
-    ('cy', 1, 2),
-    ('qb', 0, 0),
-    ('qb', 0, 1),
-    ('qb', 0, 2),
-    ('qb', 0, 3),
-    ('sb', 0),
-    ('m2', 1, 3, (0, 1, 2, 3)),
-    ('my', 1, 3),
-    ('cy', 1, 3),
-    ('m2', 2, 0, (0, 1, 2, 3)),
-    ('tb', 1, 0),
-    ('tb', 1, 1),
-    ('my', 2, 0),
-    ('cy', 2, 0),
-    ('m2', 2, 1, (0, 1, 2, 3)),
-    ('tb', 1, 2),
-    ('tb', 1, 3),
-    ('gb', 1, 0),
-    ('my', 2, 1),
-    ('gb', 1, 1),
-    ('cy', 2, 1),
-    ('m2', 2, 2, (0, 1, 2, 3)),
-    ('my', 2, 2),
-    ('cy', 2, 2),
-    ('qb', 1, 0),
-    ('qb', 1, 1),
-    ('qb', 1, 2),
-    ('qb', 1, 3),
-    ('sb', 1),
-    ('m2', 2, 3, (0, 1, 2, 3)),
-    ('my', 2, 3),
-    ('cy', 2, 3),
-    ('sbs',),
-    ('m2', 3, 0, (0, 1, 2, 3)),
-    ('my', 3, 0),
-    ('cy', 3, 0),
-    ('m2', 3, 1, (0, 1, 2, 3)),
-    ('my', 3, 1),
-    ('cy', 3, 1),
-    ('tp', 'y', 2, (0, 1)),
-    ('tp', 'y', 2, (2, 3)),
-    ('cz', 2, (0, 1), 0, 0, 128, True),
-    ('cz', 2, (2, 3), 0, 0, 128, True),
-    ('m2', 3, 2, (0, 1, 2, 3)),
-    ('my', 3, 2),
-    ('cy', 3, 2),
-    ('qy', 2, 0, 512),
-    ('sw', 2, 0, 512),
-    ('m2', 3, 3, (0, 1, 2, 3)),
-    ('tp', 'y', 3, (0, 1)),
-    ('cz', 3, (0, 1), 0, 0, 128, True),
-    ('mb', 3, 3),
-    ('my', 3, 3),
-    ('tp', 'y', 3, (2, 3), 0),
-    ('tp', 'y', 3, (2, 3), 1),
-    ('cz', 3, (2, 3), 0, 0, 64, True),
-    ('cz', 3, (2, 3), 1, 64, 128, False),
-    ('qy', 3, 0, 256),
-    ('sw', 3, 0, 256),
-    ('qy', 3, 256, 512),
-    ('sw', 3, 256, 512),
-    ('ss',),
-]
+HALVES = ((0, 1), (2, 3))
+
+OCC, NEAR, FAR_A, FAR_B = 0, 1, 2, 3
+
+SCALAR_COLUMNS = {("block", FAR_B): 320, ("grid", 0, OCC): 320, ("grid", 1, NEAR): 192}
+
+RINGS = {"rows": 3, "grouped": 5, "v_sb": 6, "paired": 10, "k_first": 3, "y_sb": 7}
+
+STAGE_1 = """
+    d2 s2 v2 d3 q2 s3 d1 A00 v3 s1 A01 v1 A02 q3 A03 S01 V01 B00 B01 q1
+    B02 B03 S00 Q01 N00 d0 N01 c00 N02 N03 V00 s0 A10 v0 A11 B10 A12 Q00 c01 B11
+    A13 q0 B12 c02 V11 S11 O00 B13 O01 m00 O02 c03 Q11 S10 O03 m01 N10 N11 m02 t00
+    c10 N12 m03 S21 A20 V10 A21 t01 V21 c11 B20 B21 Q10 u00 N13 A22 c12 Q21 A23 B22
+    c13 O10 V20 N20 u01 O11 m10 B23 O12 S20 m11 N21 A30 t10 m12 S31 A31 V31 N22 B30
+    Q20 O13 c20 B31 N23 Q31 c21 O20 m13 N30 u10 N31 V30 A32 c22 B32 m20 O21 S30 N32
+    O22 m21 t11 m22 t20 u11 A33 Q30 B33 u20 N33 h0 O23 c23 O30 O31 h1 c30 y0 m23
+    c31 y1 m30 c32 O32 m31 t21 c33 O33 m32 u21 y2 m33 t30 h2 t31 u30 y3 u31
+"""
 
 FLOPS = 2 * 512 * 2048 * (512 + 512 + 1024 + 2048)
 
@@ -315,290 +52,332 @@ def tile_thc_laplace_mp2_core_product_k6_kernel(
         ps = ctx.enter_context(tc.psum_pool(name="ps", bufs=1))
         ctx.enter_context(tc.manual_schedule())
 
-        turns = {}
-
-        def ring(pool, tag, depth, shape, dtype):
-            turn = turns.get(tag, 0)
-            turns[tag] = turn + 1
-            return pool.tile(shape, dtype, name="%s_%d" % (tag, turn), tag="%s%d" % (tag, turn % depth), align_bytes=64)
-
-        free_banks = list(range(BANKS))
-        bank_of = {}
-
-        def take_bank(key):
-            bank_of[key] = free_banks.pop(0)
-            turns["bank"] = turns.get("bank", 0) + 1
-            return ps.tile([P, W], F32, name="bank_%d" % turns["bank"], tag="bank%d" % bank_of[key])
-
-        def give_bank(key):
-            free_banks.append(bank_of[key])
-
         def keep(name, shape, dtype):
             return sb.tile(shape, dtype, name=name, align_bytes=64)
+
+        made = {}
+
+        def ring(kind, shape, dtype):
+            count = made.get(kind, 0)
+            made[kind] = count + 1
+            tag = "%s%d" % (kind, count % RINGS[kind])
+            return sb.tile(shape, dtype, name="%s_%d" % (kind, count), tag=tag, align_bytes=64)
+
+        free_banks = list(range(BANKS))
+        bank_number, bank = {}, {}
+
+        def take_bank(key):
+            bank_number[key] = free_banks.pop(0)
+            bank[key] = ps.tile([P, W], F32, name="bank_%d" % len(bank), tag="bank%d" % bank_number[key])
+
+        def give_bank(key):
+            free_banks.append(bank_number[key])
 
         def chunk(c):
             return slice(c * W, (c + 1) * W)
 
-        ident = keep("ident", [P, P], F32)
-        make_identity(nc, ident[:])
+        def tile_columns(i):
+            return slice(i * P, (i + 1) * P)
 
-        xf_sc = keep("xf_sc", [P, NCH, 2, W], U8)
-        c_sc = keep("c_sc", [P, NCH * W], U8)
-        nc.vector.memset(xf_sc[:].rearrange("p g k n -> p (g k n)").bitcast(U32), 0)
-        nc.vector.memset(c_sc[:].bitcast(U32), 0)
+        def quadrant(q, count):
+            return slice(32 * q, 32 * q + count)
 
-        eo_sb = keep("eo_sb", [P, PACK], BF16)
-        ev_sb = keep("ev_sb", [P, PACK], BF16)
-        ef_sb = keep("ef_sb", [P, 2, PACK], BF16)
-        nc.scalar.dma_start(out=ef_sb[:], in_=ef.rearrange("(g p j) -> p g j", g=2, j=PACK))
-        nc.scalar.dma_start(out=ev_sb[:], in_=ev.rearrange("(p j) -> p j", j=PACK))
-        nc.scalar.dma_start(out=eo_sb[:], in_=eo.rearrange("(p j) -> p j", j=PACK))
-        damp = keep("damp", [P, 4 * PACK], F32)
-        nc.scalar.activation(out=damp[:, 8:16], in_=ef_sb[:].rearrange("p g j -> p (g j)"), func=EXP, scale=-1.0)
-        nc.scalar.activation(out=damp[:, 4:8], in_=ev_sb[:], func=EXP, scale=-1.0)
-        nc.scalar.activation(out=damp[:, 0:4], in_=eo_sb[:], func=EXP, scale=-1.0)
+        def read_in_pair_order(ap):
+            return ap.rearrange("p (m u e) -> p u m e", u=2, e=2)
 
-        l_src = [xo_b, xv_b, xf_b[0:W, :], xf_b[W : 2 * W, :]]
-        x_src = [xo_g, xv_g]
-        l_raw, x_raw, xf_w, c_w, src_of, grouped = {}, {}, {}, {}, {}, {}
-
-        def load_l(k):
-            l_raw[k] = keep("l_raw%d" % k, [P, PACK, W], BF16)
-            nc.sync.dma_start(out=l_raw[k][:], in_=l_src[k].rearrange("(p j) b -> p j b", j=PACK))
-
-        def load_x(g, s):
-            x_raw[g, s] = keep("x_raw%d_%d" % (g, s), [P, PACK, W], BF16)
-            src_of["x", g, s] = x_raw[g, s]
-            nc.sync.dma_start(out=x_raw[g, s][:], in_=x_src[s][:, chunk(g)].rearrange("(p j) n -> p j n", j=PACK))
-
-        def load_xf(g):
-            xf_w[g] = keep("xf_w%d" % g, [P, 2, 2 * W], U8)
-            src = xf_words.rearrange("k p n -> p k n")[:, :, 2 * W * g : 2 * W * (g + 1)]
-            nc.sync.dma_start(out=xf_w[g][:].bitcast(I32), in_=src.bitcast(I32))
-
-        def load_c(n):
-            c_w[n] = keep("c_w%d" % n, [P, NCH, W], U32)
-            src = c_words.rearrange("g p n t -> p g (n t)")[:, :, PACK * W * n : PACK * W * (n + 1)]
-            nc.sync.dma_start(out=c_w[n][:].bitcast(I32), in_=src.bitcast(I32))
-
-        def load_xs(g):
-            for q in range(QUADS):
-                nc.sync.dma_start(
-                    out=xf_sc[32 * q : 32 * q + 4, g, :, :].bitcast(I32),
-                    in_=xf_scales[:, 4 * q : 4 * q + 4, chunk(g)].rearrange("k r n -> r k n").bitcast(I32),
-                )
-
-        def load_cs():
-            for q in range(QUADS):
-                nc.sync.dma_start(
-                    out=c_sc[32 * q : 32 * q + 16, :].bitcast(I32),
-                    in_=c_scales[:, 4 * q : 4 * q + 4, :].bitcast(I32),
-                )
-
-        w_sb = keep("w_sb", [P, NCH * W], BF16)
-
-        def load_w():
-            nc.sync.dma_start(out=w_sb[:], in_=w.partition_broadcast(P))
-
-        l_codes = keep("l_codes", [P, 4, W], U32)
-        l_sc = keep("l_sc", [P, 4, W], U8)
-        x_codes = keep("x_codes", [P, NCH, 2, W], U32)
-        x_sc = keep("x_sc", [P, NCH, 2, W], U8)
-        h_codes = keep("h_codes", [P, NCH, W], U32)
-        h_sc = keep("h_sc", [P, NCH, W], U8)
-        y_sc = keep("y_sc", [P, W], U8)
-        yb_sc = keep("yb_sc", [P, NBLK, P], U8)
-
-        def scale_l(k, c0, c1):
-            if ("l", k) not in src_of:
-                src_of["l", k] = ring(sb, "damped", 3, [P, PACK, W], BF16)
-            for j in range(PACK):
-                nc.vector.tensor_scalar(
-                    out=src_of["l", k][:, j, c0:c1], in0=l_raw[k][:, j, c0:c1],
-                    scalar1=damp[:, PACK * k + j : PACK * k + j + 1], scalar2=None, op0=MULT,
-                )
-
-        def interleave(key, on_scalar, c0, c1):
-            if key not in grouped:
-                grouped[key] = ring(sb, "grouped", 5, [P, W, PACK], BF16)
-            dst = grouped[key][:, c0:c1, :].rearrange("p (c i) t -> p c t i", i=4)
-            src = src_of[key][:, :, c0:c1].rearrange("p t (c i) -> p c t i", i=4)
-            if on_scalar:
-                nc.scalar.copy(out=dst, in_=src)
-            else:
-                nc.vector.tensor_copy(out=dst, in_=src)
+        def lying_in_pair_order(ap):
+            return ap.rearrange("p (u m e) -> p u m e", u=2, e=2)
 
         def quantize(codes, scales, values):
             nc.vector.quantize_mx(out=codes.bitcast(FP8X4), scales=scales, in_=values)
 
-        def quant_l(k, c0, c1):
-            quantize(l_codes[:, k, c0:c1], l_sc[:, k, c0:c1], grouped["l", k][:, c0:c1, :].rearrange("p n t -> p (n t)"))
+        ident = keep("ident", [P, P], F32)
+        make_identity(nc, ident[:])
 
-        def quant_x(g, s):
-            quantize(x_codes[:, g, s, :], x_sc[:, g, s, :], grouped["x", g, s][:].rearrange("p n t -> p (n t)"))
+        xf_planes = keep("xf_planes", [P, CHUNKS, 2, W], U8)
+        c_planes = keep("c_planes", [P, CHUNKS * W], U8)
+        nc.vector.memset(xf_planes[:].rearrange("p g k n -> p (g k n)").bitcast(U32), 0)
+        nc.vector.memset(c_planes[:].bitcast(U32), 0)
 
-        o_ps, v_ps, o_sb, y_ps, y_sb, paired, turned = {}, {}, {}, {}, {}, {}, {}
+        eo_sb = keep("eo_sb", [P, PACK], BF16)
+        ev_sb = keep("ev_sb", [P, PACK], BF16)
+        ef_sb = keep("ef_sb", [P, 2, PACK], BF16)
+        nc.scalar.dma_start(out=ef_sb[:], in_=ef.rearrange("(k p t) -> p k t", k=2, t=PACK))
+        nc.scalar.dma_start(out=ev_sb[:], in_=ev.rearrange("(p t) -> p t", t=PACK))
+        nc.scalar.dma_start(out=eo_sb[:], in_=eo.rearrange("(p t) -> p t", t=PACK))
+        damping = keep("damping", [P, 4 * PACK], F32)
+        ef_flat = ef_sb[:].rearrange("p k t -> p (k t)")
+        nc.scalar.activation(out=damping[:, PACK * FAR_A :], in_=ef_flat, func=EXP, scale=-1.0)
+        nc.scalar.activation(out=damping[:, PACK * NEAR : PACK * FAR_A], in_=ev_sb[:], func=EXP, scale=-1.0)
+        nc.scalar.activation(out=damping[:, 0 : PACK * NEAR], in_=eo_sb[:], func=EXP, scale=-1.0)
 
-        v_done = {}
+        block_source = [xo_b, xv_b, xf_b[0:W, :], xf_b[W : 2 * W, :]]
+        grid_source = [xo_g, xv_g]
+        block_raw, rows, xf_codes, c_codes = {}, {}, {}, {}
+        w_sb = keep("w_sb", [P, CHUNKS * W], BF16)
 
-        def rows(b):
-            return slice(b * P, (b + 1) * P)
+        def load_block(k):
+            block_raw[k] = keep("block_raw%d" % k, [P, PACK, W], BF16)
+            nc.sync.dma_start(out=block_raw[k][:], in_=block_source[k].rearrange("(p t) b -> p t b", t=PACK))
 
-        def mm1(g, b, k):
-            if k == 0:
-                o_ps[g, b] = take_bank(("o", g, b))
-            if k > 0:
-                v_done[g, b] = v_done.get((g, b), 0) + 1
-            if k > 0 and v_done[g, b] == 1:
-                v_ps[g, b] = take_bank(("v", g, b))
-            if k < 2:
-                rhs, rhs_scale = x_codes[:, g, k, :].bitcast(FP8X4), x_sc[:, g, k, :]
-            else:
-                rhs, rhs_scale = xf_w[g][:, k - 2, :].bitcast(FP4X4), xf_sc[:, g, k - 2, :]
-            nc.tensor.matmul_mx(
-                out=(o_ps if k == 0 else v_ps)[g, b][:],
-                lhsT=l_codes[:, k, rows(b)].bitcast(FP8X4), lhsT_scale=l_sc[:, k, rows(b)],
-                rhs=rhs, rhs_scale=rhs_scale, start=(k == 0 or v_done[g, b] == 1), stop=(k == 0 or v_done[g, b] == 3),
-            )
+        def load_grid(g, o):
+            rows["grid", g, o] = keep("grid_raw%d_%d" % (g, o), [P, PACK, W], BF16)
+            source = grid_source[o][:, chunk(g)].rearrange("(p t) n -> p t n", t=PACK)
+            nc.sync.dma_start(out=rows["grid", g, o][:], in_=source)
 
-        def mm1_tile(g, b):
-            for k in range(4):
-                mm1(g, b, k)
+        def load_xf(g):
+            for q in range(QUADS):
+                source = xf_scales[:, 4 * q : 4 * q + 4, chunk(g)].rearrange("k r n -> r k n")
+                nc.sync.dma_start(out=xf_planes[quadrant(q, 4), g, :, :].bitcast(I32), in_=source.bitcast(I32))
+            xf_codes[g] = keep("xf_codes%d" % g, [P, 2, 2 * W], U8)
+            source = xf_words.rearrange("k p n -> p k n")[:, :, 2 * W * g : 2 * W * (g + 1)]
+            nc.sync.dma_start(out=xf_codes[g][:].bitcast(I32), in_=source.bitcast(I32))
 
-        def by_pairs(ap):
-            return ap.rearrange("p (m u e) -> p u m e", u=2, e=2)
+        for k in (FAR_A, FAR_B, NEAR):
+            load_block(k)
+        load_xf(0)
+        load_grid(0, NEAR)
+        load_grid(0, OCC)
+        load_block(OCC)
+        for g in range(1, CHUNKS):
+            load_xf(g)
+            load_grid(g, NEAR)
+            load_grid(g, OCC)
+        for q in range(QUADS):
+            source = c_scales[:, 4 * q : 4 * q + 4, :]
+            nc.sync.dma_start(out=c_planes[quadrant(q, 16), :].bitcast(I32), in_=source.bitcast(I32))
+        for n in range(CHUNKS):
+            c_codes[n] = keep("c_codes%d" % n, [P, CHUNKS, W], U32)
+            source = c_words.rearrange("g p n t -> p g (n t)")[:, :, PACK * W * n : PACK * W * (n + 1)]
+            nc.sync.dma_start(out=c_codes[n][:].bitcast(I32), in_=source.bitcast(I32))
+            nc.sync.dma_start(out=w_sb[:, chunk(n)], in_=w[chunk(n)].partition_broadcast(P))
 
-        def as_pairs(ap):
-            return ap.rearrange("p (u m e) -> p u m e", u=2, e=2)
+        block_codes = keep("block_codes", [P, 4, W], U32)
+        block_planes = keep("block_planes", [P, 4, W], U8)
+        grid_codes = keep("grid_codes", [P, CHUNKS, 2, W], U32)
+        grid_planes = keep("grid_planes", [P, CHUNKS, 2, W], U8)
+        h_codes = keep("h_codes", [P, CHUNKS, W], U32)
+        h_planes = keep("h_planes", [P, CHUNKS, W], U8)
+        grouped = {}
 
-        def copy_o(g, b):
-            o_sb[g, b] = ring(sb, "o_sb", 6, [P, W], F32)
-            nc.scalar.copy(out=as_pairs(o_sb[g, b][:]), in_=by_pairs((v_ps if COPY_V else o_ps)[g, b][:]))
-            give_bank(("v" if COPY_V else "o", g, b))
+        def damp(k):
+            rows["block", k] = ring("rows", [P, PACK, W], BF16)
+            for t in range(PACK):
+                nc.vector.tensor_scalar(
+                    out=rows["block", k][:, t, :], in0=block_raw[k][:, t, :],
+                    scalar1=damping[:, PACK * k + t : PACK * k + t + 1], scalar2=None, op0=MULT,
+                )
 
-        def mul_h(g, b):
-            paired["h", g, b] = ring(sb, "paired", 10, [P, W], BF16)
-            nc.vector.tensor_tensor(
-                out=as_pairs(paired["h", g, b][:]), in0=by_pairs((o_ps if COPY_V else v_ps)[g, b][:]), in1=as_pairs(o_sb[g, b][:]), op=MULT,
-            )
-            give_bank(("o" if COPY_V else "v", g, b))
-
-        def turn(kind, c, bs, copy=0):
-            key = (kind, c, bs, copy)
-            bank = take_bank(key)
-            for i, b in enumerate(bs):
-                words = paired[kind, c, b][:].bitcast(F32)
-                for u in range(2):
-                    slot = 2 * u + i if kind == "h" else 2 * i + u
-                    nc.tensor.transpose(bank[:, slot * P : (slot + 1) * P], words[:, u * P : (u + 1) * P], ident[:])
-            turned[key] = bank
-
-        kfirst = {}
-
-        def copy_h(kind, g, bs):
-            if ("h", g) not in kfirst:
-                kfirst["h", g] = ring(sb, "kfirst", 3, [P, W * PACK], BF16)
-            dst = kfirst["h", g][:].bitcast(F32).rearrange("p (z a u) -> p z a u", z=4, u=2)
-            src = turned["h", g, bs, 0][:].rearrange("p (u a z) -> p z a u", u=2, z=4)
-            nc.scalar.copy(out=dst[:, :, 32 * bs[0] : 32 * bs[0] + 64, :], in_=src)
-            give_bank(("h", g, bs, 0))
-
-        def quant_h(g, c0, c1):
-            quantize(h_codes[:, g, c0:c1], h_sc[:, g, c0:c1], kfirst["h", g][:, PACK * c0 : PACK * c1])
-
-        def copy_y(n, bs, copy, a0, a1, on_scalar):
-            if ("y", n) not in kfirst:
-                kfirst["y", n] = ring(sb, "kfirst", 3, [P, W * PACK], BF16)
-            dst = kfirst["y", n][:].bitcast(F32).rearrange("p (a r) -> p a r", r=8)[:, a0:a1, 2 * bs[0] : 2 * bs[0] + 4]
-            src = turned["y", n, bs, copy][:].rearrange("p (r a) -> p a r", r=4)[:, a0:a1, :]
+        def lay_out(operand, on_scalar):
+            if operand not in grouped:
+                grouped[operand] = ring("grouped", [P, W, PACK], BF16)
+            split = SCALAR_COLUMNS.get(operand, W // 2)
+            columns = slice(0, split) if on_scalar else slice(split, W)
+            target = grouped[operand][:, columns, :].rearrange("p (c i) t -> p c t i", i=4)
+            source = rows[operand][:, :, columns].rearrange("p t (c i) -> p c t i", i=4)
             if on_scalar:
-                nc.scalar.copy(out=dst, in_=src)
+                nc.scalar.copy(out=target, in_=source)
             else:
-                nc.vector.tensor_copy(out=dst, in_=src)
-            give_bank(("y", n, bs, copy))
+                nc.vector.tensor_copy(out=target, in_=source)
 
-        blocks = {}
+        def quantize_block(k):
+            quantize(block_codes[:, k, :], block_planes[:, k, :], grouped["block", k][:].rearrange("p b t -> p (b t)"))
 
-        def turn_blocks(n, b):
-            if n not in blocks:
-                blocks[n] = ring(sb, "damped", 3, [P, NB * 2 * P], F32)
-            nc.vector.transpose(out=blocks[n][:, 2 * P * b : 2 * P * (b + 1)], in_=paired["y", n, b][:].bitcast(F32))
+        def quantize_grid(g, o):
+            values = grouped["grid", g, o][:].rearrange("p n t -> p (n t)")
+            quantize(grid_codes[:, g, o, :], grid_planes[:, g, o, :], values)
 
-        def gather_blocks(n, h):
-            if ("y", n) not in kfirst:
-                kfirst["y", n] = ring(sb, "kfirst", 3, [P, W * PACK], BF16)
-            dst = kfirst["y", n][:].bitcast(F32).rearrange("p (c i r) -> p c r i", i=4, r=8)
-            src = blocks[n][:].rearrange("p (r c i) -> p c r i", r=8, i=4)
-            nc.scalar.copy(out=dst[:, 16 * h : 16 * h + 16, :, :], in_=src[:, 16 * h : 16 * h + 16, :, :])
+        v_sb, paired, k_first = {}, {}, {}
 
-        y_codes = {}
-
-        def mm2(n, b, gs):
-            for g in gs:
-                if g == 0:
-                    y_ps[n, b] = take_bank(("y", n, b))
-                nc.tensor.matmul_mx(
-                    out=y_ps[n, b][:],
-                    lhsT=h_codes[:, g, rows(b)].bitcast(FP8X4), lhsT_scale=h_sc[:, g, rows(b)],
-                    rhs=c_w[n][:, g, :].bitcast(FP8X4), rhs_scale=c_sc[4 * g :, chunk(n)],
-                    start=(g == 0), stop=(g == NCH - 1),
-                )
-
-        def mul_y(n, b):
-            y_sb[n, b] = ring(sb, "y_sb", 7, [P, W], F32)
-            nc.vector.tensor_tensor(out=y_sb[n, b][:], in0=y_ps[n, b][:], in1=w_sb[:, chunk(n)], op=MULT)
-            give_bank(("y", n, b))
-            nc.sync.dma_start(out=out_0.rearrange("(p z) n -> z p n", z=NB)[b][:, chunk(n)], in_=y_sb[n, b][:])
-
-        def cast_y(n, b):
-            paired["y", n, b] = ring(sb, "paired", 10, [P, W], BF16)
-            nc.scalar.copy(out=as_pairs(paired["y", n, b][:]), in_=by_pairs(y_sb[n, b][:]))
-
-        def quant_y(n, c0, c1):
-            if n not in y_codes:
-                y_codes[n] = keep("y_codes%d" % n, [P, W], U32)
-            quantize(y_codes[n][:, c0:c1], y_sc[4 * (n - NBLK) :, c0:c1], kfirst["y", n][:, PACK * c0 : PACK * c1])
-
-        def quant_blocks(n, mh):
-            if n not in y_codes:
-                y_codes[n] = keep("y_codes%d" % n, [P, W], U32)
-            cols = slice(mh * P, (mh + 1) * P)
-            quantize(y_codes[n][:, cols], yb_sc[4 * mh :, n, :], kfirst["y", n][:, mh * W : (mh + 1) * W])
-
-        def store_words(n, c0, c1):
-            dst = out_1[n].rearrange("p m t -> p (m t)").bitcast(I32)
-            nc.sync.dma_start(out=dst[:, c0:c1], in_=y_codes[n][:, c0:c1].bitcast(I32))
-
-        def store_block_words(n):
-            dst = out_1[n].rearrange("p m t -> p (m t)").bitcast(I32).rearrange("(h l) b -> l h b", l=32)
-            for q in range(QUADS):
-                src = y_codes[n][32 * q : 32 * q + 32, :].bitcast(I32).rearrange("l (h b) -> l h b", b=P)
-                nc.sync.dma_start(out=dst[:, :, q * P : (q + 1) * P], in_=src)
-
-        def store_block_scales():
-            for q in range(QUADS):
-                dst = out_2[0:NBLK, :, q * P : (q + 1) * P].rearrange("n r b -> r n b")
-                nc.sync.dma_start(out=dst.bitcast(I32), in_=yb_sc[32 * q : 32 * q + 16, :, :].bitcast(I32))
-
-        def mul_y_bf16(n, b):
-            paired["y", n, b] = ring(sb, "paired", 10, [P, W], BF16)
-            nc.vector.tensor_tensor(
-                out=as_pairs(paired["y", n, b][:]), in0=by_pairs(y_ps[n, b][:]), in1=by_pairs(w_sb[:, chunk(n)]), op=MULT,
+        def pass_1(k, g, i):
+            key = ("o" if k == OCC else "v", g, i)
+            if k in (OCC, FAR_A):
+                take_bank(key)
+            if k in (OCC, NEAR):
+                moving, moving_plane = grid_codes[:, g, k, :].bitcast(FP8X4), grid_planes[:, g, k, :]
+            else:
+                moving, moving_plane = xf_codes[g][:, k - FAR_A, :].bitcast(FP4X4), xf_planes[:, g, k - FAR_A, :]
+            nc.tensor.matmul_mx(
+                out=bank[key][:],
+                lhsT=block_codes[:, k, tile_columns(i)].bitcast(FP8X4), lhsT_scale=block_planes[:, k, tile_columns(i)],
+                rhs=moving, rhs_scale=moving_plane, start=k in (OCC, FAR_A), stop=k in (OCC, NEAR),
             )
 
-        def store_scales():
-            for q in range(QUADS):
-                eng = nc.sync if q % 2 else nc.scalar
-                eng.dma_start(
-                    out=out_2[NBLK:NCH, 4 * q : 4 * q + 4, :].bitcast(I32),
-                    in_=y_sc[32 * q : 32 * q + 4 * (NCH - NBLK), :].bitcast(I32),
+        def copy_v(g, i):
+            v_sb[g, i] = ring("v_sb", [P, W], F32)
+            nc.scalar.copy(out=lying_in_pair_order(v_sb[g, i][:]), in_=read_in_pair_order(bank["v", g, i][:]))
+            give_bank(("v", g, i))
+
+        def multiply_h(g, i):
+            paired["h", g, i] = ring("paired", [P, W], BF16)
+            nc.vector.tensor_tensor(
+                out=lying_in_pair_order(paired["h", g, i][:]), in0=read_in_pair_order(bank["o", g, i][:]),
+                in1=lying_in_pair_order(v_sb[g, i][:]), op=MULT,
+            )
+            give_bank(("o", g, i))
+
+        def transpose_words(key, source, slots):
+            take_bank(key)
+            for j in range(2):
+                words = source[j][:].bitcast(F32)
+                for u in range(2):
+                    nc.tensor.transpose(bank[key][:, tile_columns(slots[j][u])], words[:, tile_columns(u)], ident[:])
+
+        def transpose_h(g, h):
+            transpose_words(("ht", g, h), [paired["h", g, i] for i in HALVES[h]], ((0, 2), (1, 3)))
+
+        def copy_h(g, h):
+            if h == 0:
+                k_first["h", g] = ring("k_first", [P, W * PACK], BF16)
+            target = k_first["h", g][:].bitcast(F32).rearrange("p (z a u) -> p z a u", z=TILES, u=2)
+            source = bank["ht", g, h][:].rearrange("p (u a z) -> p z a u", u=2, z=TILES)
+            nc.scalar.copy(out=target[:, :, 64 * h : 64 * (h + 1), :], in_=source)
+            give_bank(("ht", g, h))
+
+        def quantize_h(g):
+            quantize(h_codes[:, g, :], h_planes[:, g, :], k_first["h", g][:])
+
+        y_sb = {}
+        y_rows = out_0.rearrange("(p z) n -> z p n", z=TILES)
+        y_codes = [keep("y_codes%d" % n, [P, W], U32) for n in range(CHUNKS)]
+        y_planes = [keep("y_planes%d" % n, [P, W], U8) for n in range(3)]
+        words_out = [out_1[n].rearrange("p b t -> p (b t)").bitcast(I32) for n in range(CHUNKS)]
+
+        def passes_2(n, z, chunks_of_h):
+            for g in chunks_of_h:
+                if g == 0:
+                    take_bank(("y", n, z))
+                nc.tensor.matmul_mx(
+                    out=bank["y", n, z][:],
+                    lhsT=h_codes[:, g, tile_columns(z)].bitcast(FP8X4), lhsT_scale=h_planes[:, g, tile_columns(z)],
+                    rhs=c_codes[n][:, g, :].bitcast(FP8X4), rhs_scale=c_planes[4 * g :, chunk(n)],
+                    start=(g == 0), stop=(g == CHUNKS - 1),
                 )
+
+        def finish_y(n, z):
+            y_sb[n, z] = ring("y_sb", [P, W], F32)
+            nc.vector.tensor_tensor(out=y_sb[n, z][:], in0=bank["y", n, z][:], in1=w_sb[:, chunk(n)], op=MULT)
+            give_bank(("y", n, z))
+            nc.sync.dma_start(out=y_rows[z][:, chunk(n)], in_=y_sb[n, z][:])
+
+        def round_y(n, z, target):
+            paired["y", n, z] = target
+            nc.scalar.copy(out=lying_in_pair_order(target[:]), in_=read_in_pair_order(y_sb[n, z][:]))
+
+        def transpose_y(n, h, name="yt"):
+            transpose_words((name, n, h), [paired["y", n, z] for z in HALVES[h]], ((0, 1), (2, 3)))
+
+        def copy_y(copy, n, h, points, name="yt"):
+            if ("y", n) not in k_first:
+                k_first["y", n] = ring("k_first", [P, W * PACK], BF16)
+            target = k_first["y", n][:].bitcast(F32).rearrange("m (p r) -> m p r", r=8)[:, points, 4 * h : 4 * (h + 1)]
+            copy(out=target, in_=bank[name, n, h][:].rearrange("m (r p) -> m p r", r=4)[:, points, :])
+            give_bank((name, n, h))
+
+        def quantize_y(n, columns):
+            plane = y_planes[2][4:, columns] if n == 3 else y_planes[n][:, columns]
+            quantize(y_codes[n][:, columns], plane, k_first["y", n][:, PACK * columns.start : PACK * columns.stop])
+
+        def store_words(n, columns):
+            nc.sync.dma_start(out=words_out[n][:, columns], in_=y_codes[n][:, columns].bitcast(I32))
 
         steps = {
-            "sl": scale_l, "il": interleave, "ql": quant_l, "qx": quant_x, "m1": mm1, "co": copy_o, "mh": mul_h,
-            "tp": turn, "ct": copy_h, "cz": copy_y, "tb": turn_blocks, "gb": gather_blocks, "qb": quant_blocks, "sb": store_block_words, "sbs": store_block_scales, "qh": quant_h, "m2": mm2, "my": mul_y, "cy": cast_y, "qy": quant_y,
-            "lx": load_x, "ll": load_l, "lf": load_xf, "lc": load_c, "ls": load_xs, "lcs": load_cs, "lw": load_w,
-            "sw": store_words, "mb": mul_y_bf16, "ss": store_scales,
+            "d": damp, "q": quantize_block, "Q": quantize_grid, "c": copy_v, "m": multiply_h,
+            "t": transpose_h, "u": copy_h, "h": quantize_h,
+            "s": lambda k: lay_out(("block", k), True), "v": lambda k: lay_out(("block", k), False),
+            "S": lambda g, o: lay_out(("grid", g, o), True), "V": lambda g, o: lay_out(("grid", g, o), False),
+            "O": lambda g, i: pass_1(OCC, g, i), "N": lambda g, i: pass_1(NEAR, g, i),
+            "A": lambda g, i: pass_1(FAR_A, g, i), "B": lambda g, i: pass_1(FAR_B, g, i),
+            "y": lambda z: passes_2(0, z, (0, 1)),
         }
-        for step in ORDER:
-            steps[step[0]](*step[1:])
+        for step in STAGE_1.split():
+            steps[step[0]](*[int(digit) for digit in step[1:]])
+
+        for z in range(TILES):
+            passes_2(0, z, (2,))
+        quantize_h(3)
+        passes_2(1, 0, (0, 1, 2))
+
+        paired_0 = ring("grouped", [P, TILES * W], BF16)
+        for z in range(TILES):
+            passes_2(0, z, (3,))
+            finish_y(0, z)
+            round_y(0, z, paired_0[:, chunk(z)])
+        blocks_0 = ring("rows", [P, TILES * W // 2], F32)
+
+        def turn_blocks(h):
+            nc.vector.transpose(out=blocks_0[:, chunk(h)], in_=paired_0[:].bitcast(F32)[:, chunk(h)])
+
+        def gather_blocks():
+            k_first["y", 0] = ring("k_first", [P, W * PACK], BF16)
+            target = k_first["y", 0][:].bitcast(F32).rearrange("p (c i r) -> p c r i", i=4, r=8)
+            nc.scalar.copy(out=target, in_=blocks_0[:].rearrange("p (r c i) -> p c r i", r=8, i=4))
+
+        def store_planes_0():
+            quantize_y(0, slice(0, W))
+            for q in range(QUADS):
+                target = words_out[0].rearrange("(a l) b -> l a b", l=32)[:, :, tile_columns(q)]
+                source = y_codes[0][quadrant(q, 32), :].bitcast(I32).rearrange("l (a b) -> l a b", b=P)
+                nc.sync.dma_start(out=target, in_=source)
+            for q in range(QUADS):
+                target = out_2[0, :, tile_columns(q)].rearrange("(a r) b -> r a b", r=4)
+                source = y_planes[0][quadrant(q, 4), :].rearrange("r (a b) -> r a b", b=P)
+                nc.sync.dma_start(out=target.bitcast(I32), in_=source.bitcast(I32))
+
+        def tile_2(n, z):
+            passes_2(n, z, (3,) if (n, z) == (1, 0) else range(CHUNKS))
+            finish_y(n, z)
+            round_y(n, z, ring("paired", [P, W], BF16))
+
+        tile_2(1, 0)
+        tile_2(1, 1)
+        turn_blocks(0)
+        tile_2(1, 2)
+        turn_blocks(1)
+        gather_blocks()
+        tile_2(1, 3)
+        tile_2(2, 0)
+        store_planes_0()
+        for z in range(1, TILES):
+            tile_2(2, z)
+
+        passes_2(3, 0, range(CHUNKS))
+        finish_y(3, 0)
+        for n in (1, 2):
+            for h in range(2):
+                transpose_y(n, h)
+        for n in (1, 2):
+            for h in range(2):
+                copy_y(nc.scalar.copy, n, h, slice(0, P))
+        round_y(3, 0, ring("paired", [P, W], BF16))
+        quantize_y(1, slice(0, W))
+        store_words(1, slice(0, W))
+        for q in range(QUADS):
+            target = out_2[1, 4 * q : 4 * q + 4, :]
+            nc.sync.dma_start(out=target.bitcast(I32), in_=y_planes[1][quadrant(q, 4), :].bitcast(I32))
+        tile_2(3, 1)
+        quantize_y(2, slice(0, W))
+        store_words(2, slice(0, W))
+        tile_2(3, 2)
+
+        passes_2(3, 3, range(CHUNKS))
+        transpose_y(3, 0)
+        copy_y(nc.scalar.copy, 3, 0, slice(0, P))
+        paired["y", 3, 3] = ring("paired", [P, W], BF16)
+        nc.vector.tensor_tensor(
+            out=lying_in_pair_order(paired["y", 3, 3][:]), in0=read_in_pair_order(bank["y", 3, 3][:]),
+            in1=read_in_pair_order(w_sb[:, chunk(3)]), op=MULT,
+        )
+        finish_y(3, 3)
+        transpose_y(3, 1)
+        transpose_y(3, 1, "yt again")
+        copy_y(nc.scalar.copy, 3, 1, slice(0, P // 2))
+        copy_y(nc.vector.tensor_copy, 3, 1, slice(P // 2, P), "yt again")
+        quantize_y(3, slice(0, W // 2))
+        store_words(3, slice(0, W // 2))
+        quantize_y(3, slice(W // 2, W))
+        for q in range(QUADS):
+            queue = nc.sync if q % 2 else nc.scalar
+            target = out_2[2:CHUNKS, 4 * q : 4 * q + 4, :]
+            queue.dma_start(out=target.bitcast(I32), in_=y_planes[2][quadrant(q, 8), :].bitcast(I32))
+        store_words(3, slice(W // 2, W))

from contextlib import ExitStack

import concourse.mybir as mybir
from concourse.masks import make_identity

F32 = mybir.dt.float32
BF16 = mybir.dt.bfloat16
I32 = mybir.dt.int32
U32 = mybir.dt.uint32
U8 = mybir.dt.uint8
FP8X4 = mybir.dt.float8_e4m3fn_x4
FP4X4 = mybir.dt.float4_e2m1fn_x4
MULT = mybir.AluOpType.mult
EXP = mybir.ActivationFunctionType.Exp

P = 128
PACK = 4
W = 512
CHUNKS = 4
TILES = 4
QUADS = 4
BANKS = 8
HALVES = ((0, 1), (2, 3))

OCC, NEAR, FAR_A, FAR_B = 0, 1, 2, 3

SCALAR_COLUMNS = {("block", FAR_B): 320, ("grid", 0, OCC): 320, ("grid", 1, NEAR): 192}

RINGS = {"rows": 3, "grouped": 5, "v_sb": 6, "paired": 10, "k_first": 3, "y_sb": 7}

STAGE_1 = """
    d2 s2 v2 d3 q2 s3 d1 A00 v3 s1 A01 v1 A02 q3 A03 S01 V01 B00 B01 q1
    B02 B03 S00 Q01 N00 d0 N01 c00 N02 N03 V00 s0 A10 v0 A11 B10 A12 Q00 c01 B11
    A13 q0 B12 c02 V11 S11 O00 B13 O01 m00 O02 c03 Q11 S10 O03 m01 N10 N11 m02 t00
    c10 N12 m03 S21 A20 V10 A21 t01 V21 c11 B20 B21 Q10 u00 N13 A22 c12 Q21 A23 B22
    c13 O10 V20 N20 u01 O11 m10 B23 O12 S20 m11 N21 A30 t10 m12 S31 A31 V31 N22 B30
    Q20 O13 c20 B31 N23 Q31 c21 O20 m13 N30 u10 N31 V30 A32 c22 B32 m20 O21 S30 N32
    O22 m21 t11 m22 t20 u11 A33 Q30 B33 u20 N33 h0 O23 c23 O30 O31 h1 c30 y0 m23
    c31 y1 m30 c32 O32 m31 t21 c33 O33 m32 u21 y2 m33 t30 h2 t31 u30 y3 u31
"""

FLOPS = 2 * 512 * 2048 * (512 + 512 + 1024 + 2048)


def tile_thc_laplace_mp2_core_product_k6_kernel(
    tc, xo_b, xo_g, eo, xv_b, xv_g, ev, xf_b, xf_words, xf_scales, ef, c_words, c_scales, w,
    out_0, out_1, out_2,
):
    nc = tc.nc
    with ExitStack() as ctx:
        sb = ctx.enter_context(tc.tile_pool(name="sb", bufs=1))
        ps = ctx.enter_context(tc.psum_pool(name="ps", bufs=1))
        ctx.enter_context(tc.manual_schedule())

        def keep(name, shape, dtype):
            return sb.tile(shape, dtype, name=name, align_bytes=64)

        made = {}

        def ring(kind, shape, dtype):
            count = made.get(kind, 0)
            made[kind] = count + 1
            tag = "%s%d" % (kind, count % RINGS[kind])
            return sb.tile(shape, dtype, name="%s_%d" % (kind, count), tag=tag, align_bytes=64)

        free_banks = list(range(BANKS))
        bank_number, bank = {}, {}

        def take_bank(key):
            bank_number[key] = free_banks.pop(0)
            bank[key] = ps.tile([P, W], F32, name="bank_%d" % len(bank), tag="bank%d" % bank_number[key])

        def give_bank(key):
            free_banks.append(bank_number[key])

        def chunk(c):
            return slice(c * W, (c + 1) * W)

        def tile_columns(i):
            return slice(i * P, (i + 1) * P)

        def quadrant(q, count):
            return slice(32 * q, 32 * q + count)

        def read_in_pair_order(ap):
            return ap.rearrange("p (m u e) -> p u m e", u=2, e=2)

        def lying_in_pair_order(ap):
            return ap.rearrange("p (u m e) -> p u m e", u=2, e=2)

        def quantize(codes, scales, values):
            nc.vector.quantize_mx(out=codes.bitcast(FP8X4), scales=scales, in_=values)

        ident = keep("ident", [P, P], F32)
        make_identity(nc, ident[:])

        xf_planes = keep("xf_planes", [P, CHUNKS, 2, W], U8)
        c_planes = keep("c_planes", [P, CHUNKS * W], U8)
        nc.vector.memset(xf_planes[:].rearrange("p g k n -> p (g k n)").bitcast(U32), 0)
        nc.vector.memset(c_planes[:].bitcast(U32), 0)

        eo_sb = keep("eo_sb", [P, PACK], BF16)
        ev_sb = keep("ev_sb", [P, PACK], BF16)
        ef_sb = keep("ef_sb", [P, 2, PACK], BF16)
        nc.scalar.dma_start(out=ef_sb[:], in_=ef.rearrange("(k p t) -> p k t", k=2, t=PACK))
        nc.scalar.dma_start(out=ev_sb[:], in_=ev.rearrange("(p t) -> p t", t=PACK))
        nc.scalar.dma_start(out=eo_sb[:], in_=eo.rearrange("(p t) -> p t", t=PACK))
        damping = keep("damping", [P, 4 * PACK], F32)
        ef_flat = ef_sb[:].rearrange("p k t -> p (k t)")
        nc.scalar.activation(out=damping[:, PACK * FAR_A :], in_=ef_flat, func=EXP, scale=-1.0)
        nc.scalar.activation(out=damping[:, PACK * NEAR : PACK * FAR_A], in_=ev_sb[:], func=EXP, scale=-1.0)
        nc.scalar.activation(out=damping[:, 0 : PACK * NEAR], in_=eo_sb[:], func=EXP, scale=-1.0)

        block_source = [xo_b, xv_b, xf_b[0:W, :], xf_b[W : 2 * W, :]]
        grid_source = [xo_g, xv_g]
        block_raw, rows, xf_codes, c_codes = {}, {}, {}, {}
        w_sb = keep("w_sb", [P, CHUNKS * W], BF16)

        def load_block(k):
            block_raw[k] = keep("block_raw%d" % k, [P, PACK, W], BF16)
            nc.sync.dma_start(out=block_raw[k][:], in_=block_source[k].rearrange("(p t) b -> p t b", t=PACK))

        def load_grid(g, o):
            rows["grid", g, o] = keep("grid_raw%d_%d" % (g, o), [P, PACK, W], BF16)
            source = grid_source[o][:, chunk(g)].rearrange("(p t) n -> p t n", t=PACK)
            nc.sync.dma_start(out=rows["grid", g, o][:], in_=source)

        def load_xf(g):
            for q in range(QUADS):
                source = xf_scales[:, 4 * q : 4 * q + 4, chunk(g)].rearrange("k r n -> r k n")
                nc.sync.dma_start(out=xf_planes[quadrant(q, 4), g, :, :].bitcast(I32), in_=source.bitcast(I32))
            xf_codes[g] = keep("xf_codes%d" % g, [P, 2, 2 * W], U8)
            source = xf_words.rearrange("k p n -> p k n")[:, :, 2 * W * g : 2 * W * (g + 1)]
            nc.sync.dma_start(out=xf_codes[g][:].bitcast(I32), in_=source.bitcast(I32))

        for k in (FAR_A, FAR_B, NEAR):
            load_block(k)
        load_xf(0)
        load_grid(0, NEAR)
        load_grid(0, OCC)
        load_block(OCC)
        for g in range(1, CHUNKS):
            load_xf(g)
            load_grid(g, NEAR)
            load_grid(g, OCC)
        for q in range(QUADS):
            source = c_scales[:, 4 * q : 4 * q + 4, :]
            nc.sync.dma_start(out=c_planes[quadrant(q, 16), :].bitcast(I32), in_=source.bitcast(I32))
        for n in range(CHUNKS):
            c_codes[n] = keep("c_codes%d" % n, [P, CHUNKS, W], U32)
            source = c_words.rearrange("g p n t -> p g (n t)")[:, :, PACK * W * n : PACK * W * (n + 1)]
            nc.sync.dma_start(out=c_codes[n][:].bitcast(I32), in_=source.bitcast(I32))
            nc.sync.dma_start(out=w_sb[:, chunk(n)], in_=w[chunk(n)].partition_broadcast(P))

        block_codes = keep("block_codes", [P, 4, W], U32)
        block_planes = keep("block_planes", [P, 4, W], U8)
        grid_codes = keep("grid_codes", [P, CHUNKS, 2, W], U32)
        grid_planes = keep("grid_planes", [P, CHUNKS, 2, W], U8)
        h_codes = keep("h_codes", [P, CHUNKS, W], U32)
        h_planes = keep("h_planes", [P, CHUNKS, W], U8)
        grouped = {}

        def damp(k):
            rows["block", k] = ring("rows", [P, PACK, W], BF16)
            for t in range(PACK):
                nc.vector.tensor_scalar(
                    out=rows["block", k][:, t, :], in0=block_raw[k][:, t, :],
                    scalar1=damping[:, PACK * k + t : PACK * k + t + 1], scalar2=None, op0=MULT,
                )

        def lay_out(operand, on_scalar):
            if operand not in grouped:
                grouped[operand] = ring("grouped", [P, W, PACK], BF16)
            split = SCALAR_COLUMNS.get(operand, W // 2)
            columns = slice(0, split) if on_scalar else slice(split, W)
            target = grouped[operand][:, columns, :].rearrange("p (c i) t -> p c t i", i=4)
            source = rows[operand][:, :, columns].rearrange("p t (c i) -> p c t i", i=4)
            if on_scalar:
                nc.scalar.copy(out=target, in_=source)
            else:
                nc.vector.tensor_copy(out=target, in_=source)

        def quantize_block(k):
            quantize(block_codes[:, k, :], block_planes[:, k, :], grouped["block", k][:].rearrange("p b t -> p (b t)"))

        def quantize_grid(g, o):
            values = grouped["grid", g, o][:].rearrange("p n t -> p (n t)")
            quantize(grid_codes[:, g, o, :], grid_planes[:, g, o, :], values)

        v_sb, paired, k_first = {}, {}, {}

        def pass_1(k, g, i):
            key = ("o" if k == OCC else "v", g, i)
            if k in (OCC, FAR_A):
                take_bank(key)
            if k in (OCC, NEAR):
                moving, moving_plane = grid_codes[:, g, k, :].bitcast(FP8X4), grid_planes[:, g, k, :]
            else:
                moving, moving_plane = xf_codes[g][:, k - FAR_A, :].bitcast(FP4X4), xf_planes[:, g, k - FAR_A, :]
            nc.tensor.matmul_mx(
                out=bank[key][:],
                lhsT=block_codes[:, k, tile_columns(i)].bitcast(FP8X4), lhsT_scale=block_planes[:, k, tile_columns(i)],
                rhs=moving, rhs_scale=moving_plane, start=k in (OCC, FAR_A), stop=k in (OCC, NEAR),
            )

        def copy_v(g, i):
            v_sb[g, i] = ring("v_sb", [P, W], F32)
            nc.scalar.copy(out=lying_in_pair_order(v_sb[g, i][:]), in_=read_in_pair_order(bank["v", g, i][:]))
            give_bank(("v", g, i))

        def multiply_h(g, i):
            paired["h", g, i] = ring("paired", [P, W], BF16)
            nc.vector.tensor_tensor(
                out=lying_in_pair_order(paired["h", g, i][:]), in0=read_in_pair_order(bank["o", g, i][:]),
                in1=lying_in_pair_order(v_sb[g, i][:]), op=MULT,
            )
            give_bank(("o", g, i))

        def transpose_words(key, source, slots):
            take_bank(key)
            for j in range(2):
                words = source[j][:].bitcast(F32)
                for u in range(2):
                    nc.tensor.transpose(bank[key][:, tile_columns(slots[j][u])], words[:, tile_columns(u)], ident[:])

        def transpose_h(g, h):
            transpose_words(("ht", g, h), [paired["h", g, i] for i in HALVES[h]], ((0, 2), (1, 3)))

        def copy_h(g, h):
            if h == 0:
                k_first["h", g] = ring("k_first", [P, W * PACK], BF16)
            target = k_first["h", g][:].bitcast(F32).rearrange("p (z a u) -> p z a u", z=TILES, u=2)
            source = bank["ht", g, h][:].rearrange("p (u a z) -> p z a u", u=2, z=TILES)
            nc.scalar.copy(out=target[:, :, 64 * h : 64 * (h + 1), :], in_=source)
            give_bank(("ht", g, h))

        def quantize_h(g):
            quantize(h_codes[:, g, :], h_planes[:, g, :], k_first["h", g][:])

        y_sb = {}
        y_rows = out_0.rearrange("(p z) n -> z p n", z=TILES)
        y_codes = [keep("y_codes%d" % n, [P, W], U32) for n in range(CHUNKS)]
        y_planes = [keep("y_planes%d" % n, [P, W], U8) for n in range(3)]
        words_out = [out_1[n].rearrange("p b t -> p (b t)").bitcast(I32) for n in range(CHUNKS)]

        def passes_2(n, z, chunks_of_h):
            for g in chunks_of_h:
                if g == 0:
                    take_bank(("y", n, z))
                nc.tensor.matmul_mx(
                    out=bank["y", n, z][:],
                    lhsT=h_codes[:, g, tile_columns(z)].bitcast(FP8X4), lhsT_scale=h_planes[:, g, tile_columns(z)],
                    rhs=c_codes[n][:, g, :].bitcast(FP8X4), rhs_scale=c_planes[4 * g :, chunk(n)],
                    start=(g == 0), stop=(g == CHUNKS - 1),
                )

        def finish_y(n, z):
            y_sb[n, z] = ring("y_sb", [P, W], F32)
            nc.vector.tensor_tensor(out=y_sb[n, z][:], in0=bank["y", n, z][:], in1=w_sb[:, chunk(n)], op=MULT)
            give_bank(("y", n, z))
            nc.sync.dma_start(out=y_rows[z][:, chunk(n)], in_=y_sb[n, z][:])

        def round_y(n, z, target):
            paired["y", n, z] = target
            nc.scalar.copy(out=lying_in_pair_order(target[:]), in_=read_in_pair_order(y_sb[n, z][:]))

        def transpose_y(n, h, name="yt"):
            transpose_words((name, n, h), [paired["y", n, z] for z in HALVES[h]], ((0, 1), (2, 3)))

        def copy_y(copy, n, h, points, name="yt"):
            if ("y", n) not in k_first:
                k_first["y", n] = ring("k_first", [P, W * PACK], BF16)
            target = k_first["y", n][:].bitcast(F32).rearrange("m (p r) -> m p r", r=8)[:, points, 4 * h : 4 * (h + 1)]
            copy(out=target, in_=bank[name, n, h][:].rearrange("m (r p) -> m p r", r=4)[:, points, :])
            give_bank((name, n, h))

        def quantize_y(n, columns):
            plane = y_planes[2][4:, columns] if n == 3 else y_planes[n][:, columns]
            quantize(y_codes[n][:, columns], plane, k_first["y", n][:, PACK * columns.start : PACK * columns.stop])

        def store_words(n, columns):
            nc.sync.dma_start(out=words_out[n][:, columns], in_=y_codes[n][:, columns].bitcast(I32))

        steps = {
            "d": damp, "q": quantize_block, "Q": quantize_grid, "c": copy_v, "m": multiply_h,
            "t": transpose_h, "u": copy_h, "h": quantize_h,
            "s": lambda k: lay_out(("block", k), True), "v": lambda k: lay_out(("block", k), False),
            "S": lambda g, o: lay_out(("grid", g, o), True), "V": lambda g, o: lay_out(("grid", g, o), False),
            "O": lambda g, i: pass_1(OCC, g, i), "N": lambda g, i: pass_1(NEAR, g, i),
            "A": lambda g, i: pass_1(FAR_A, g, i), "B": lambda g, i: pass_1(FAR_B, g, i),
            "y": lambda z: passes_2(0, z, (0, 1)),
        }
        for step in STAGE_1.split():
            steps[step[0]](*[int(digit) for digit in step[1:]])

        for z in range(TILES):
            passes_2(0, z, (2,))
        quantize_h(3)
        passes_2(1, 0, (0, 1, 2))

        paired_0 = ring("grouped", [P, TILES * W], BF16)
        for z in range(TILES):
            passes_2(0, z, (3,))
            finish_y(0, z)
            round_y(0, z, paired_0[:, chunk(z)])
        blocks_0 = ring("rows", [P, TILES * W // 2], F32)

        def turn_blocks(h):
            nc.vector.transpose(out=blocks_0[:, chunk(h)], in_=paired_0[:].bitcast(F32)[:, chunk(h)])

        def gather_blocks():
            k_first["y", 0] = ring("k_first", [P, W * PACK], BF16)
            target = k_first["y", 0][:].bitcast(F32).rearrange("p (c i r) -> p c r i", i=4, r=8)
            nc.scalar.copy(out=target, in_=blocks_0[:].rearrange("p (r c i) -> p c r i", r=8, i=4))

        def store_planes_0():
            quantize_y(0, slice(0, W))
            for q in range(QUADS):
                target = words_out[0].rearrange("(a l) b -> l a b", l=32)[:, :, tile_columns(q)]
                source = y_codes[0][quadrant(q, 32), :].bitcast(I32).rearrange("l (a b) -> l a b", b=P)
                nc.sync.dma_start(out=target, in_=source)
            for q in range(QUADS):
                target = out_2[0, :, tile_columns(q)].rearrange("(a r) b -> r a b", r=4)
                source = y_planes[0][quadrant(q, 4), :].rearrange("r (a b) -> r a b", b=P)
                nc.sync.dma_start(out=target.bitcast(I32), in_=source.bitcast(I32))

        def tile_2(n, z):
            passes_2(n, z, (3,) if (n, z) == (1, 0) else range(CHUNKS))
            finish_y(n, z)
            round_y(n, z, ring("paired", [P, W], BF16))

        tile_2(1, 0)
        tile_2(1, 1)
        turn_blocks(0)
        tile_2(1, 2)
        turn_blocks(1)
        gather_blocks()
        tile_2(1, 3)
        tile_2(2, 0)
        store_planes_0()
        for z in range(1, TILES):
            tile_2(2, z)

        passes_2(3, 0, range(CHUNKS))
        finish_y(3, 0)
        for n in (1, 2):
            for h in range(2):
                transpose_y(n, h)
        for n in (1, 2):
            for h in range(2):
                copy_y(nc.scalar.copy, n, h, slice(0, P))
        round_y(3, 0, ring("paired", [P, W], BF16))
        quantize_y(1, slice(0, W))
        store_words(1, slice(0, W))
        for q in range(QUADS):
            target = out_2[1, 4 * q : 4 * q + 4, :]
            nc.sync.dma_start(out=target.bitcast(I32), in_=y_planes[1][quadrant(q, 4), :].bitcast(I32))
        tile_2(3, 1)
        quantize_y(2, slice(0, W))
        store_words(2, slice(0, W))
        tile_2(3, 2)

        passes_2(3, 3, range(CHUNKS))
        transpose_y(3, 0)
        copy_y(nc.scalar.copy, 3, 0, slice(0, P))
        paired["y", 3, 3] = ring("paired", [P, W], BF16)
        nc.vector.tensor_tensor(
            out=lying_in_pair_order(paired["y", 3, 3][:]), in0=read_in_pair_order(bank["y", 3, 3][:]),
            in1=read_in_pair_order(w_sb[:, chunk(3)]), op=MULT,
        )
        finish_y(3, 3)
        transpose_y(3, 1)
        transpose_y(3, 1, "yt again")
        copy_y(nc.scalar.copy, 3, 1, slice(0, P // 2))
        copy_y(nc.vector.tensor_copy, 3, 1, slice(P // 2, P), "yt again")
        quantize_y(3, slice(0, W // 2))
        store_words(3, slice(0, W // 2))
        quantize_y(3, slice(W // 2, W))
        for q in range(QUADS):
            queue = nc.sync if q % 2 else nc.scalar
            target = out_2[2:CHUNKS, 4 * q : 4 * q + 4, :]
            queue.dma_start(out=target.bitcast(I32), in_=y_planes[2][quadrant(q, 8), :].bitcast(I32))
        store_words(3, slice(W // 2, W))
